import numpy as np
import ml_dtypes


def mxq(x, axis, fmt="e4m3"):
    dtype, down = {"e4m3": (ml_dtypes.float8_e4m3fn, 7), "e5m2": (ml_dtypes.float8_e5m2, 14)}[fmt]
    v = np.moveaxis(np.asarray(x, np.float32).astype(ml_dtypes.bfloat16).astype(np.float64), axis, -1)
    blocks = v.reshape(v.shape[:-1] + (-1, 32))
    amax = np.abs(blocks).max(-1, keepdims=True)
    byte = np.maximum(np.where(amax > 0, np.frexp(amax)[1] - 1 + 127, 0) - down, 1)
    scale = np.exp2(byte - 127.0)
    codes = (blocks / scale).astype(np.float32).astype(dtype).astype(np.float64)
    return np.moveaxis((codes * scale).reshape(v.shape), -1, axis)


WIDE = False


def mx_kscale(k):
    if not WIDE:
        return np.ones(k)
    levels = np.array([10, -10, 5, -5, 0])
    if k % 512:
        return np.exp2(np.random.permutation(np.resize(levels, k // 32))).repeat(32)
    a = np.empty((k // 512, 16))
    for p in range(k // 512):
        a[p, :8] = np.random.permutation(np.resize(levels, 8))
        for g in range(8):
            far = levels[np.abs(levels - a[p, g]) >= 10]
            a[p, g + 8] = far[np.random.randint(len(far))]
    return np.exp2(a.ravel()).repeat(32)


def f64(x):
    return np.asarray(x).astype(np.float64)


def striped(idx):
    return np.tile(np.asarray(idx).reshape(-1, 16).T, (8, 1)).astype(np.uint16)


def unstriped(offs):
    return offs[:16].T.reshape(-1).astype(np.int64)


B, N, T, D, DV, NQ = 2, 512, 2048, 512, 512, 128
PAGE = 64


def setup_inputs():
    n = np.random.standard_normal
    pages = np.random.permutation(T // PAGE)[:B * N // PAGE]
    idx = (pages[:, None] * PAGE + np.arange(PAGE)[None, :]).reshape(-1)
    s = mx_kscale(D)[:, None]
    u = np.ones(T)
    u[idx] = mx_kscale(B * N)
    r = np.random.uniform(0.5, 2.0, T)
    raw = n((D, T)) / s / (u * r)
    return {
        "qT": (n((B, D, NQ)) * s * (1.00 / np.sqrt(D))).astype(np.float32),
        "cT": raw.astype(np.float32),
        "ts": np.tile(u * r, (128, 1)).astype(np.float32),
        "ch": np.tile(s[:, 0] * np.random.uniform(0.5, 2.0, D), (128, 1)).astype(np.float32),
        "offs": striped(idx),
    }


def reference(qT, cT, ts, ch, offs):
    idx = unstriped(offs)
    c = f64(cT)
    pick = lambda x: x[:, idx].reshape(x.shape[0], B, N).transpose(1, 0, 2)
    q = f64(qT)
    score = mxq(q, 1, "e4m3").transpose(0, 2, 1) @ mxq(pick(c), 1, "e4m3")
    score = score * pick(f64(ts))[:, :1, :]
    m = score.max(-1, keepdims=True)
    p = np.exp(score - m)
    total = p.sum(-1, keepdims=True)
    w = p * pick(f64(ts))[:, :1, :]
    y = mxq(w, 2, "e4m3") @ mxq(pick(c).transpose(0, 2, 1), 1, "e4m3")
    y = y / total
    y = y * f64(ch)[:1]
    return y

@@ -1,0 +1,284 @@
+from contextlib import ExitStack
+
+import concourse.mybir as mybir
+from concourse.masks import make_identity
+
+B, N, T, D, DV, NQ = 2, 512, 2048, 512, 512, 128
+P = 128
+PACK = 4
+FLOPS = 2 * B * NQ * N * (D + DV)
+
+F32 = mybir.dt.float32
+BF16 = mybir.dt.bfloat16
+U32 = mybir.dt.uint32
+U16 = mybir.dt.uint16
+U8 = mybir.dt.uint8
+FP8X4 = mybir.dt.float8_e4m3fn_x4
+ACT = mybir.ActivationFunctionType
+ALU = mybir.AluOpType
+
+CHUNKS = [(0, 0, 1024, 688), (0, 1024, 1024, 688), (1, 0, 512, 0), (1, 512, 1024, 1024), (1, 1536, 512, 512)]
+
+
+def tile_attend_mla_kernel(tc, qT, cT, ts, ch, offs, out):
+    nc = tc.nc
+    with ExitStack() as ctx:
+        keep = ctx.enter_context(tc.tile_pool(name="keep", bufs=1))
+        psum = ctx.enter_context(tc.psum_pool(name="psum", bufs=1))
+
+        offsets = keep.tile([P, B * N // 16], U16, name="offsets")
+        nc.sync.dma_start(offsets[:], offs)
+        lists = [offsets[:, b * (N // 16) : (b + 1) * (N // 16)] for b in range(B)]
+        pool_rows = cT.rearrange("(p t) n -> p t n", t=PACK)
+        raw = []
+        for i, (u, c0, w, wv) in enumerate(CHUNKS):
+            r = keep.tile([P, 2, w], F32, name=f"raw{i}")
+            nc.sync.dma_start(out=r[:], in_=pool_rows[:, 2 * u : 2 * u + 2, c0 : c0 + w])
+            raw.append(r)
+        q_raw = keep.tile([P, B, PACK, NQ], F32, name="q_raw")
+        nc.sync.dma_start(out=q_raw[:], in_=qT.rearrange("b (p t) q -> p b t q", t=PACK))
+        ts_sb = keep.tile([P, T], F32, name="ts_sb")
+        nc.sync.dma_start(out=ts_sb[:], in_=ts)
+        ch_sb = keep.tile([P, DV], F32, name="ch_sb")
+        nc.sync.dma_start(out=ch_sb[:], in_=ch)
+
+        ident_f = keep.tile([P, P], F32, name="ident_f")
+        make_identity(nc, ident_f[:])
+        warm = keep.tile([P, 1], F32, name="warm")
+        nc.gpsimd.memset(warm[:], 0.0)
+        warm2 = keep.tile([P, 1], F32, name="warm2")
+        nc.scalar.activation(out=warm2[:], in_=warm[:], func=ACT.Exp)
+
+        words = [keep.tile([P, T, 2], BF16, name=f"words{u}") for u in range(2)]
+        picked = [keep.tile([P, 2, N, 2], BF16, name=f"picked{b}") for b in range(B)]
+        keys = [keep.tile([P, N, 2, 2], BF16, name=f"keys{b}", align_bytes=64) for b in range(B)]
+        kq = [keep.tile([P, N], U32, name=f"kq{b}", align_bytes=64) for b in range(B)]
+        ks = [keep.tile([P, N], U8, name=f"ks{b}", align_bytes=64) for b in range(B)]
+        vals = [keep.tile([P, DV, 4], BF16, name=f"vals{b}", align_bytes=64) for b in range(B)]
+        q_sb = keep.tile([P, B, NQ, PACK], BF16, name="q_sb", align_bytes=64)
+        qq = keep.tile([P, B * NQ], U32, name="qq", align_bytes=64)
+        qs = keep.tile([P, B * NQ], U8, name="qs", align_bytes=64)
+        toks = keep.tile([P, B, N], F32, name="toks", tag="toks", align_bytes=64)
+        turned, scores, tts, tcol, a, neg_m, p, total, pts, wts, wqs, invs, ys, vqs = ({} for i in range(14))
+
+        def cv(i):
+            u, c0, w, wv = CHUNKS[i]
+            nc.vector.tensor_copy(
+                out=words[u][:, c0 : c0 + wv, :], in_=raw[i][:, :, 0:wv].rearrange("p e n -> p n e")
+            )
+
+        def cs(i):
+            u, c0, w, wv = CHUNKS[i]
+            nc.scalar.activation(
+                out=words[u][:, c0 + wv : c0 + w, :],
+                in_=raw[i][:, :, wv:w].rearrange("p e n -> p n e"),
+                func=ACT.Copy,
+            )
+
+        def g(b, u):
+            nc.vector.tensor_copy(
+                out=picked[b][:, u].rearrange("p n e -> p (n e)").bitcast(U32),
+                in_=words[u][:].rearrange("p n e -> p (n e)").bitcast(U32).indirect(lists[b]),
+            )
+
+        def tv(b, u):
+            t = psum.tile([P, 4, P], F32, name="turned", bufs=4)
+            pairs = picked[b][:, u].rearrange("p n e -> p (n e)").bitcast(F32).rearrange("p (s j) -> p j s", j=4)
+            for j in range(4):
+                nc.tensor.transpose(t[:, j, :], pairs[:, j, :], ident_f[:])
+            turned[b, u] = t
+
+        def vc(b, u):
+            nc.scalar.copy(
+                out=vals[b][:, u * 2 * P : (u + 1) * 2 * P, :].rearrange("s (e p) j -> s e p j", e=2),
+                in_=turned[b, u][:].rearrange("s j p -> s (j p)").bitcast(BF16).rearrange("s (j p e) -> s e p j", j=4, e=2),
+            )
+
+        def qv(b):
+            if "vq" not in vqs:
+                vqs["vq"] = keep.tile([P, B, DV], U32, name="vq", tag="toks", align_bytes=64)
+                vqs["vs"] = keep.tile([P, B, DV], U8, name="vs", align_bytes=64)
+            nc.vector.quantize_mx(
+                out=vqs["vq"][:, b, :].bitcast(FP8X4),
+                scales=vqs["vs"][:, b, :],
+                in_=vals[b][:].rearrange("p c j -> p (c j)"),
+            )
+
+        def qc(b):
+            nc.scalar.activation(out=q_sb[:, b], in_=q_raw[:, b].rearrange("p t q -> p q t"), func=ACT.Copy)
+
+        def qQ():
+            nc.vector.quantize_mx(
+                out=qq[:].bitcast(FP8X4), scales=qs[:], in_=q_sb[:].rearrange("p b q t -> p (b q t)")
+            )
+
+        def ilv(b):
+            if b == 0:
+                nc.vector.tensor_copy(
+                    out=keys[b][:].rearrange("p n u e -> p (n u e)").bitcast(F32).rearrange("p (n u) -> p n u", u=2),
+                    in_=picked[b][:].rearrange("p u n e -> p (u n e)").bitcast(F32).rearrange("p (u n) -> p n u", u=2),
+                )
+            else:
+                nc.scalar.copy(out=keys[b][:], in_=picked[b][:].rearrange("p u n e -> p n u e"))
+
+        def qK(b):
+            nc.vector.quantize_mx(
+                out=kq[b][:].bitcast(FP8X4), scales=ks[b][:], in_=keys[b][:].rearrange("p n u e -> p (n u e)")
+            )
+
+        def mm(b):
+            sc = psum.tile([P, N], F32, name="sc", tag="sc", bufs=2)
+            nc.tensor.matmul_mx(
+                out=sc[:],
+                lhsT=qq[:, b * NQ : (b + 1) * NQ].bitcast(FP8X4),
+                lhsT_scale=qs[:, b * NQ : (b + 1) * NQ],
+                rhs=kq[b][:].bitcast(FP8X4),
+                rhs_scale=ks[b][:],
+                start=True,
+                stop=True,
+            )
+            scores[b] = sc
+
+        def tok(b):
+            nc.vector.tensor_copy(out=toks[:, b, :], in_=ts_sb[:].indirect(lists[b]))
+
+        def tt(b):
+            t = psum.tile([P, 4, P], F32, name="tt", tag="pt", bufs=2)
+            for j in range(4):
+                nc.tensor.transpose(t[:, j, :], toks[:, b, :].rearrange("q (s j) -> q j s", j=4)[:, j, :], ident_f[:])
+            tts[b] = t
+
+        def tcl(b):
+            tcol[b] = keep.tile([P, 4], F32, name=f"tcol{b}")
+            nc.scalar.copy(out=tcol[b][:], in_=tts[b][:, :, 0])
+
+        def sca(b):
+            a[b] = keep.tile([P, N], F32, name=f"a{b}")
+            nc.vector.tensor_tensor(out=a[b][:], in0=scores[b][:], in1=toks[:, b, :], op=ALU.mult)
+
+        def mx(b):
+            neg_m[b] = keep.tile([P, 1], F32, name=f"nm{b}")
+            nc.vector.tensor_reduce(
+                out=neg_m[b][:],
+                in_=a[b][:],
+                axis=mybir.AxisListType.X,
+                op=ALU.max,
+                negate=True,
+            )
+
+        def ex(b):
+            p[b] = keep.tile([P, 4, P], F32, name=f"p{b}")
+            total[b] = keep.tile([P, 1], F32, name=f"total{b}")
+            nc.scalar.activation(
+                out=p[b][:].rearrange("q j s -> q s j"),
+                in_=a[b][:].rearrange("q (s j) -> q s j", j=4),
+                func=ACT.Exp,
+                bias=neg_m[b][:],
+                scale=1.0,
+                accum_out=total[b][:],
+            )
+
+        def pt(b):
+            t = psum.tile([P, 4, P], F32, name="pt", tag="pt", bufs=2)
+            for j in range(4):
+                nc.tensor.transpose(t[:, j, :], p[b][:, j, :], ident_f[:])
+            pts[b] = t
+
+        def w(b):
+            wts[b] = keep.tile([P, NQ, 4], BF16, name=f"w{b}", align_bytes=64)
+            nc.vector.tensor_tensor(
+                out=wts[b][:],
+                in0=pts[b][:].rearrange("s j q -> s q j"),
+                in1=tcol[b][:].unsqueeze(1).to_broadcast([P, NQ, 4]),
+                op=ALU.mult,
+            )
+
+        def qw(b):
+            wq = keep.tile([P, NQ], U32, name=f"wq{b}", align_bytes=64)
+            ws = keep.tile([P, NQ], U8, name=f"ws{b}", align_bytes=64)
+            nc.vector.quantize_mx(out=wq[:].bitcast(FP8X4), scales=ws[:], in_=wts[b][:].rearrange("s q j -> s (q j)"))
+            wqs[b] = (wq, ws)
+
+        def rec(b):
+            invs[b] = keep.tile([P, 1], F32, name=f"inv{b}")
+            nc.vector.reciprocal(out=invs[b][:], in_=total[b][:])
+
+        def mix(b):
+            wq, ws = wqs[b]
+            ys[b] = psum.tile([P, DV], F32, name="y", tag="sc", bufs=2)
+            nc.tensor.matmul_mx(
+                out=ys[b][:],
+                lhsT=wq[:].bitcast(FP8X4),
+                lhsT_scale=ws[:],
+                rhs=vqs["vq"][:, b, :].bitcast(FP8X4),
+                rhs_scale=vqs["vs"][:, b, :],
+                start=True,
+                stop=True,
+            )
+
+        def fin(b):
+            o = keep.tile([P, DV], F32, name=f"o{b}")
+            nc.vector.scalar_tensor_tensor(
+                out=o[:].rearrange("q (p f) -> q p f", f=4),
+                in0=ys[b][:].rearrange("q (f p) -> q p f", f=4),
+                scalar=invs[b][:],
+                in1=ch_sb[:].rearrange("q (p f) -> q p f", f=4),
+                op0=ALU.mult,
+                op1=ALU.mult,
+            )
+            nc.sync.dma_start(out=out[b], in_=o[:])
+
+        cv(0)
+        cs(0)
+        cv(1)
+        cs(1)
+        g(0, 0)
+        cs(2)
+        g(1, 0)
+        tv(0, 0)
+        vc(0, 0)
+        cv(3)
+        tv(1, 0)
+        vc(1, 0)
+        cv(4)
+        qc(0)
+        qc(1)
+        g(0, 1)
+        g(1, 1)
+        ilv(1)
+        ilv(0)
+        tv(0, 1)
+        vc(0, 1)
+        tv(1, 1)
+        vc(1, 1)
+        qQ()
+        qK(0)
+        mm(0)
+        qK(1)
+        mm(1)
+        tok(0)
+        tt(0)
+        tcl(0)
+        tok(1)
+        tt(1)
+        tcl(1)
+        sca(0)
+        sca(1)
+        mx(0)
+        ex(0)
+        mx(1)
+        ex(1)
+        pt(0)
+        rec(0)
+        w(0)
+        pt(1)
+        qw(0)
+        qv(0)
+        mix(0)
+        w(1)
+        rec(1)
+        qw(1)
+        qv(1)
+        mix(1)
+        fin(0)
+        fin(1)

@@ -11,13 +11,14 @@ FLOPS = 2 * B * NQ * N * (D + DV)
 F32 = mybir.dt.float32
 BF16 = mybir.dt.bfloat16
 U32 = mybir.dt.uint32
+I32 = mybir.dt.int32
 U16 = mybir.dt.uint16
 U8 = mybir.dt.uint8
 FP8X4 = mybir.dt.float8_e4m3fn_x4
 ACT = mybir.ActivationFunctionType
 ALU = mybir.AluOpType
 
-CHUNKS = [(0, 0, 1024, 688), (0, 1024, 1024, 688), (1, 0, 512, 0), (1, 512, 1024, 1024), (1, 1536, 512, 512)]
+CHUNKS = [(0, 0, 512, 0), (0, 512, 512, 0), (0, 1024, 768, 512), (0, 1792, 256, 256), (1, 0, 512, 0), (1, 512, 768, 768), (1, 1280, 512, 512), (1, 1792, 256, 256)]
 
 
 def tile_attend_mla_kernel(tc, qT, cT, ts, ch, offs, out):
@@ -29,16 +30,22 @@ def tile_attend_mla_kernel(tc, qT, cT, ts, ch, offs, out):
         offsets = keep.tile([P, B * N // 16], U16, name="offsets")
         nc.sync.dma_start(offsets[:], offs)
         lists = [offsets[:, b * (N // 16) : (b + 1) * (N // 16)] for b in range(B)]
+        ts_sb = keep.tile([P, T], F32, name="ts_sb")
+        nc.gpsimd.memset(ts_sb[:, 0 : T // 2], 0.0)
+        nc.vector.memset(ts_sb[:, T // 2 : T], 0.0)
         pool_rows = cT.rearrange("(p t) n -> p t n", t=PACK)
         raw = []
         for i, (u, c0, w, wv) in enumerate(CHUNKS):
-            r = keep.tile([P, 2, w], F32, name=f"raw{i}")
+            r = keep.tile([P, 2, w], F32, name=f"raw{i}", tag=f"raw{i}", align_bytes=64)
             nc.sync.dma_start(out=r[:], in_=pool_rows[:, 2 * u : 2 * u + 2, c0 : c0 + w])
             raw.append(r)
-        q_raw = keep.tile([P, B, PACK, NQ], F32, name="q_raw")
-        nc.sync.dma_start(out=q_raw[:], in_=qT.rearrange("b (p t) q -> p b t q", t=PACK))
-        ts_sb = keep.tile([P, T], F32, name="ts_sb")
-        nc.sync.dma_start(out=ts_sb[:], in_=ts)
+            if i == 0:
+                nc.sync.dma_start(out=ts_sb[0:1, :], in_=ts[0:1, :])
+        q_raw = []
+        for b in range(B):
+            r = keep.tile([P, PACK, NQ], F32, name=f"q_raw{b}")
+            nc.sync.dma_start(out=r[:], in_=qT[b].rearrange("(p t) q -> p t q", t=PACK))
+            q_raw.append(r)
         ch_sb = keep.tile([P, DV], F32, name="ch_sb")
         nc.sync.dma_start(out=ch_sb[:], in_=ch)
 
@@ -51,15 +58,17 @@ def tile_attend_mla_kernel(tc, qT, cT, ts, ch, offs, out):
 
         words = [keep.tile([P, T, 2], BF16, name=f"words{u}") for u in range(2)]
         picked = [keep.tile([P, 2, N, 2], BF16, name=f"picked{b}") for b in range(B)]
-        keys = [keep.tile([P, N, 2, 2], BF16, name=f"keys{b}", align_bytes=64) for b in range(B)]
+        keys = {}
         kq = [keep.tile([P, N], U32, name=f"kq{b}", align_bytes=64) for b in range(B)]
         ks = [keep.tile([P, N], U8, name=f"ks{b}", align_bytes=64) for b in range(B)]
-        vals = [keep.tile([P, DV, 4], BF16, name=f"vals{b}", align_bytes=64) for b in range(B)]
+        vals = {}
         q_sb = keep.tile([P, B, NQ, PACK], BF16, name="q_sb", align_bytes=64)
         qq = keep.tile([P, B * NQ], U32, name="qq", align_bytes=64)
         qs = keep.tile([P, B * NQ], U8, name="qs", align_bytes=64)
-        toks = keep.tile([P, B, N], F32, name="toks", tag="toks", align_bytes=64)
-        turned, scores, tts, tcol, a, neg_m, p, total, pts, wts, wqs, invs, ys, vqs = ({} for i in range(14))
+        toks = keep.tile([P, B, N], F32, name="toks", align_bytes=64)
+        trow = [keep.tile([P, N], F32, name=f"trow{b}", tag=f"trow{b}", align_bytes=64) for b in range(B)]
+        vs = keep.tile([P, B, DV], U8, name="vs", align_bytes=64)
+        turned, scores, tts, tcol, a, neg_m, p, total, pts, wts, wqs, invs, ys = ({} for i in range(13))
 
         def cv(i):
             u, c0, w, wv = CHUNKS[i]
@@ -77,49 +86,56 @@ def tile_attend_mla_kernel(tc, qT, cT, ts, ch, offs, out):
 
         def g(b, u):
             nc.vector.tensor_copy(
-                out=picked[b][:, u].rearrange("p n e -> p (n e)").bitcast(U32),
+                out=picked[b][:, u].rearrange("p n e -> p (n e)").bitcast(U32).rearrange("p (j s) -> p s j", j=4),
                 in_=words[u][:].rearrange("p n e -> p (n e)").bitcast(U32).indirect(lists[b]),
             )
 
         def tv(b, u):
             t = psum.tile([P, 4, P], F32, name="turned", bufs=4)
-            pairs = picked[b][:, u].rearrange("p n e -> p (n e)").bitcast(F32).rearrange("p (s j) -> p j s", j=4)
+            pairs = picked[b][:, u].rearrange("p n e -> p (n e)").bitcast(F32).rearrange("p (j s) -> p j s", j=4)
             for j in range(4):
                 nc.tensor.transpose(t[:, j, :], pairs[:, j, :], ident_f[:])
             turned[b, u] = t
 
         def vc(b, u):
+            if (b, u) == (0, 0):
+                both = keep.tile([P, B, 2 * P, 4], BF16, name="vals_first", tag="raw4", align_bytes=64)
+                vals[0, 0], vals[1, 0] = both[:, 0], both[:, 1]
+            if (b, u) == (0, 1):
+                vals[b, u] = keep.tile([P, 2 * P, 4], BF16, name="vals01", align_bytes=64)[:]
+            if (b, u) == (1, 1):
+                vals[b, u] = keep.tile([P, 2 * P, 4], BF16, name="vals11", align_bytes=64)[:]
             nc.scalar.copy(
-                out=vals[b][:, u * 2 * P : (u + 1) * 2 * P, :].rearrange("s (e p) j -> s e p j", e=2),
+                out=vals[b, u].rearrange("s (e p) j -> s e p j", e=2),
                 in_=turned[b, u][:].rearrange("s j p -> s (j p)").bitcast(BF16).rearrange("s (j p e) -> s e p j", j=4, e=2),
             )
 
-        def qv(b):
-            if "vq" not in vqs:
-                vqs["vq"] = keep.tile([P, B, DV], U32, name="vq", tag="toks", align_bytes=64)
-                vqs["vs"] = keep.tile([P, B, DV], U8, name="vs", align_bytes=64)
+        def qv(b, u):
+            cols = slice(u * 2 * P, (u + 1) * 2 * P)
+            if "vq" not in vals:
+                vals["vq"] = keep.tile([P, B, DV], U32, name="vq", tag="trow1", align_bytes=64)
             nc.vector.quantize_mx(
-                out=vqs["vq"][:, b, :].bitcast(FP8X4),
-                scales=vqs["vs"][:, b, :],
-                in_=vals[b][:].rearrange("p c j -> p (c j)"),
+                out=vals["vq"][:, b, cols].bitcast(FP8X4),
+                scales=vs[:, b, cols],
+                in_=vals[b, u].rearrange("p c j -> p (c j)"),
             )
 
         def qc(b):
-            nc.scalar.activation(out=q_sb[:, b], in_=q_raw[:, b].rearrange("p t q -> p q t"), func=ACT.Copy)
+            nc.scalar.activation(out=q_sb[:, b], in_=q_raw[b][:].rearrange("p t q -> p q t"), func=ACT.Copy)
 
-        def qQ():
+        def qQ(b):
+            cols = slice(b * NQ, (b + 1) * NQ)
             nc.vector.quantize_mx(
-                out=qq[:].bitcast(FP8X4), scales=qs[:], in_=q_sb[:].rearrange("p b q t -> p (b q t)")
+                out=qq[:, cols].bitcast(FP8X4), scales=qs[:, cols], in_=q_sb[:, b].rearrange("p q t -> p (q t)")
             )
 
         def ilv(b):
-            if b == 0:
-                nc.vector.tensor_copy(
-                    out=keys[b][:].rearrange("p n u e -> p (n u e)").bitcast(F32).rearrange("p (n u) -> p n u", u=2),
-                    in_=picked[b][:].rearrange("p u n e -> p (u n e)").bitcast(F32).rearrange("p (u n) -> p n u", u=2),
-                )
-            else:
-                nc.scalar.copy(out=keys[b][:], in_=picked[b][:].rearrange("p u n e -> p n u e"))
+            keys[b] = keep.tile([P, N, 2, 2], BF16, name=f"keys{b}", tag="keys", align_bytes=64)
+            copy, word = (nc.scalar.copy, U32) if b == 0 else (nc.vector.tensor_copy, I32)
+            copy(
+                out=keys[b][:].rearrange("p n u e -> p (n u e)").bitcast(word).rearrange("p (n u) -> p n u", u=2),
+                in_=picked[b][:].rearrange("p u n e -> p (u n e)").bitcast(word).rearrange("p (u n) -> p n u", u=2),
+            )
 
         def qK(b):
             nc.vector.quantize_mx(
@@ -139,8 +155,8 @@ def tile_attend_mla_kernel(tc, qT, cT, ts, ch, offs, out):
             )
             scores[b] = sc
 
-        def tok(b):
-            nc.vector.tensor_copy(out=toks[:, b, :], in_=ts_sb[:].indirect(lists[b]))
+        def tok():
+            nc.vector.tensor_copy(out=toks[:].rearrange("p b n -> p (b n)"), in_=ts_sb[:].indirect(offsets[:]))
 
         def tt(b):
             t = psum.tile([P, 4, P], F32, name="tt", tag="pt", bufs=2)
@@ -149,12 +165,20 @@ def tile_attend_mla_kernel(tc, qT, cT, ts, ch, offs, out):
             tts[b] = t
 
         def tcl(b):
-            tcol[b] = keep.tile([P, 4], F32, name=f"tcol{b}")
-            nc.scalar.copy(out=tcol[b][:], in_=tts[b][:, :, 0])
+            if b == 0:
+                both = keep.tile([P, B, 4], F32, name="tcols", tag="raw2", align_bytes=64)
+                tcol[0], tcol[1] = both[:, 0], both[:, 1]
+            nc.scalar.copy(out=tcol[b], in_=tts[b][:, :, 0])
+
+        def spread(b):
+            t = psum.tile([P, 4, P], F32, name="sp", tag="pt", bufs=2)
+            for j in range(4):
+                nc.tensor.transpose(t[:, j, :], tcol[b][:, j : j + 1].to_broadcast([P, P]), ident_f[:])
+            nc.scalar.copy(out=trow[b][:], in_=t[:].rearrange("q j s -> q (j s)"))
 
         def sca(b):
-            a[b] = keep.tile([P, N], F32, name=f"a{b}")
-            nc.vector.tensor_tensor(out=a[b][:], in0=scores[b][:], in1=toks[:, b, :], op=ALU.mult)
+            a[b] = keep.tile([P, N], F32, name=f"a{b}", tag=f"a{b}", align_bytes=64)
+            nc.vector.tensor_tensor(out=a[b][:], in0=scores[b][:], in1=trow[b][:], op=ALU.mult)
 
         def mx(b):
             neg_m[b] = keep.tile([P, 1], F32, name=f"nm{b}")
@@ -170,8 +194,8 @@ def tile_attend_mla_kernel(tc, qT, cT, ts, ch, offs, out):
             p[b] = keep.tile([P, 4, P], F32, name=f"p{b}")
             total[b] = keep.tile([P, 1], F32, name=f"total{b}")
             nc.scalar.activation(
-                out=p[b][:].rearrange("q j s -> q s j"),
-                in_=a[b][:].rearrange("q (s j) -> q s j", j=4),
+                out=p[b][:].rearrange("q j s -> q (j s)"),
+                in_=a[b][:],
                 func=ACT.Exp,
                 bias=neg_m[b][:],
                 scale=1.0,
@@ -189,7 +213,7 @@ def tile_attend_mla_kernel(tc, qT, cT, ts, ch, offs, out):
             nc.vector.tensor_tensor(
                 out=wts[b][:],
                 in0=pts[b][:].rearrange("s j q -> s q j"),
-                in1=tcol[b][:].unsqueeze(1).to_broadcast([P, NQ, 4]),
+                in1=tcol[b].unsqueeze(1).to_broadcast([P, NQ, 4]),
                 op=ALU.mult,
             )
 
@@ -210,8 +234,8 @@ def tile_attend_mla_kernel(tc, qT, cT, ts, ch, offs, out):
                 out=ys[b][:],
                 lhsT=wq[:].bitcast(FP8X4),
                 lhsT_scale=ws[:],
-                rhs=vqs["vq"][:, b, :].bitcast(FP8X4),
-                rhs_scale=vqs["vs"][:, b, :],
+                rhs=vals["vq"][:, b, :].bitcast(FP8X4),
+                rhs_scale=vs[:, b, :],
                 start=True,
                 stop=True,
             )
@@ -228,57 +252,63 @@ def tile_attend_mla_kernel(tc, qT, cT, ts, ch, offs, out):
             )
             nc.sync.dma_start(out=out[b], in_=o[:])
 
-        cv(0)
+        tok()
         cs(0)
-        cv(1)
         cs(1)
-        g(0, 0)
+        cv(2)
         cs(2)
+        tt(0)
+        tt(1)
+        cv(3)
+        g(0, 0)
+        tcl(0)
+        tcl(1)
+        spread(0)
+        spread(1)
+        cs(4)
         g(1, 0)
         tv(0, 0)
         vc(0, 0)
-        cv(3)
         tv(1, 0)
+        cv(5)
+        cv(6)
         vc(1, 0)
-        cv(4)
-        qc(0)
-        qc(1)
+        cv(7)
         g(0, 1)
-        g(1, 1)
-        ilv(1)
+        qc(0)
         ilv(0)
-        tv(0, 1)
-        vc(0, 1)
-        tv(1, 1)
-        vc(1, 1)
-        qQ()
+        g(1, 1)
+        qQ(0)
         qK(0)
         mm(0)
+        ilv(1)
+        qc(1)
+        qQ(1)
         qK(1)
         mm(1)
-        tok(0)
-        tt(0)
-        tcl(0)
-        tok(1)
-        tt(1)
-        tcl(1)
+        tv(0, 1)
+        tv(1, 1)
+        vc(0, 1)
         sca(0)
-        sca(1)
         mx(0)
         ex(0)
+        sca(1)
         mx(1)
         ex(1)
+        vc(1, 1)
         pt(0)
-        rec(0)
         w(0)
         pt(1)
+        qv(0, 0)
+        qv(0, 1)
         qw(0)
-        qv(0)
         mix(0)
         w(1)
-        rec(1)
+        qv(1, 0)
+        qv(1, 1)
         qw(1)
-        qv(1)
         mix(1)
+        rec(0)
+        rec(1)
         fin(0)
         fin(1)

@@ -6,6 +6,7 @@ from concourse.masks import make_identity
 B, N, T, D, DV, NQ = 2, 512, 2048, 512, 512, 128
 P = 128
 PACK = 4
+H = 2
 FLOPS = 2 * B * NQ * N * (D + DV)
 
 F32 = mybir.dt.float32
@@ -18,21 +19,30 @@ FP8X4 = mybir.dt.float8_e4m3fn_x4
 ACT = mybir.ActivationFunctionType
 ALU = mybir.AluOpType
 
-CHUNKS = [(0, 0, 512, 0), (0, 512, 512, 0), (0, 1024, 768, 512), (0, 1792, 256, 256), (1, 0, 512, 0), (1, 512, 768, 768), (1, 1280, 512, 512), (1, 1792, 256, 256)]
+CHUNKS = [(0, 0, 640, 0), (0, 640, 640, 0), (0, 1280, 512, 512), (0, 1792, 256, 256), (1, 0, 384, 0), (1, 384, 768, 768), (1, 1152, 640, 640), (1, 1792, 256, 256)]
 
 
 def tile_attend_mla_kernel(tc, qT, cT, ts, ch, offs, out):
     nc = tc.nc
     with ExitStack() as ctx:
         keep = ctx.enter_context(tc.tile_pool(name="keep", bufs=1))
+        reuse = ctx.enter_context(tc.tile_pool(name="reuse", bufs=1))
         psum = ctx.enter_context(tc.psum_pool(name="psum", bufs=1))
+
+        warm = keep.tile([P, 1], F32, name="warm")
+        nc.vector.memset(warm[:], 0.0)
+        warm2 = keep.tile([P, 1], F32, name="warm2")
+        nc.scalar.activation(out=warm2[:], in_=warm[:], func=ACT.Exp)
+        ts_sb = keep.tile([P, T], F32, name="ts_sb")
+        nc.gpsimd.memset(ts_sb[:, T // 2 : T], 0.0)
+        nc.vector.memset(ts_sb[:, 0 : T // 2 - 1], 0.0)
+        nc.vector.memset(ts_sb[:, T // 2 - 1 : T // 2], 0.0)
+        ident_f = keep.tile([P, P], F32, name="ident_f")
+        make_identity(nc, ident_f[:])
 
         offsets = keep.tile([P, B * N // 16], U16, name="offsets")
         nc.sync.dma_start(offsets[:], offs)
         lists = [offsets[:, b * (N // 16) : (b + 1) * (N // 16)] for b in range(B)]
-        ts_sb = keep.tile([P, T], F32, name="ts_sb")
-        nc.gpsimd.memset(ts_sb[:, 0 : T // 2], 0.0)
-        nc.vector.memset(ts_sb[:, T // 2 : T], 0.0)
         pool_rows = cT.rearrange("(p t) n -> p t n", t=PACK)
         raw = []
         for i, (u, c0, w, wv) in enumerate(CHUNKS):
@@ -41,34 +51,30 @@ def tile_attend_mla_kernel(tc, qT, cT, ts, ch, offs, out):
             raw.append(r)
             if i == 0:
                 nc.sync.dma_start(out=ts_sb[0:1, :], in_=ts[0:1, :])
-        q_raw = []
+        q_both = reuse.tile([P, B * PACK * NQ], F32, name="q_both", offset=1024)
+        q_raw = [q_both[:, b * PACK * NQ : (b + 1) * PACK * NQ].rearrange("p (t q) -> p t q", t=PACK) for b in range(B)]
         for b in range(B):
-            r = keep.tile([P, PACK, NQ], F32, name=f"q_raw{b}")
-            nc.sync.dma_start(out=r[:], in_=qT[b].rearrange("(p t) q -> p t q", t=PACK))
-            q_raw.append(r)
+            nc.sync.dma_start(out=q_raw[b], in_=qT[b].rearrange("(p t) q -> p t q", t=PACK))
         ch_sb = keep.tile([P, DV], F32, name="ch_sb")
         nc.sync.dma_start(out=ch_sb[:], in_=ch)
 
-        ident_f = keep.tile([P, P], F32, name="ident_f")
-        make_identity(nc, ident_f[:])
-        warm = keep.tile([P, 1], F32, name="warm")
-        nc.gpsimd.memset(warm[:], 0.0)
-        warm2 = keep.tile([P, 1], F32, name="warm2")
-        nc.scalar.activation(out=warm2[:], in_=warm[:], func=ACT.Exp)
-
         words = [keep.tile([P, T, 2], BF16, name=f"words{u}") for u in range(2)]
-        picked = [keep.tile([P, 2, N, 2], BF16, name=f"picked{b}") for b in range(B)]
-        keys = {}
+        pick2 = [keep.tile([P, 2, N], U32, name=f"pick{b}", tag=f"pick{b}", align_bytes=64) for b in range(B)]
         kq = [keep.tile([P, N], U32, name=f"kq{b}", align_bytes=64) for b in range(B)]
         ks = [keep.tile([P, N], U8, name=f"ks{b}", align_bytes=64) for b in range(B)]
-        vals = {}
-        q_sb = keep.tile([P, B, NQ, PACK], BF16, name="q_sb", align_bytes=64)
+        vals = {0: keep.tile([P, B * 1024], BF16, name="vals0", align_bytes=64)}
+        q_sb = reuse.tile([P, B, NQ, PACK], BF16, name="q_sb", align_bytes=64, offset=6144)
         qq = keep.tile([P, B * NQ], U32, name="qq", align_bytes=64)
         qs = keep.tile([P, B * NQ], U8, name="qs", align_bytes=64)
-        toks = keep.tile([P, B, N], F32, name="toks", align_bytes=64)
-        trow = [keep.tile([P, N], F32, name=f"trow{b}", tag=f"trow{b}", align_bytes=64) for b in range(B)]
+        toks = [keep.tile([P, N], F32, name=f"toks{b}") for b in range(B)]
+        tcol = [keep.tile([P, 4], F32, name=f"tcol{b}") for b in range(B)]
         vs = keep.tile([P, B, DV], U8, name="vs", align_bytes=64)
-        turned, scores, tts, tcol, a, neg_m, p, total, pts, wts, wqs, invs, ys = ({} for i in range(13))
+        a = [keep.tile([P, 4, P], F32, name=f"a{b}") for b in range(B)]
+        p = [keep.tile([P, 4, P], F32, name=f"p{b}") for b in range(B)]
+        parts = keep.tile([P, B, H], F32, name="parts")
+        total = keep.tile([P, B], F32, name="total")
+        inv = keep.tile([P, B], F32, name="inv")
+        turned, scores, tts, neg_m, pts, wts, wqs, ys, late, keys = ({} for i in range(10))
 
         def cv(i):
             u, c0, w, wv = CHUNKS[i]
@@ -84,136 +90,149 @@ def tile_attend_mla_kernel(tc, qT, cT, ts, ch, offs, out):
                 func=ACT.Copy,
             )
 
+        def window(u):
+            return words[u][:].rearrange("p n e -> p (n e)").bitcast(U32)
+
         def g(b, u):
             nc.vector.tensor_copy(
-                out=picked[b][:, u].rearrange("p n e -> p (n e)").bitcast(U32).rearrange("p (j s) -> p s j", j=4),
-                in_=words[u][:].rearrange("p n e -> p (n e)").bitcast(U32).indirect(lists[b]),
+                out=pick2[b][:, u].rearrange("p (j s) -> p s j", j=4), in_=window(u).indirect(lists[b])
+            )
+
+        def gh(b, h):
+            nc.vector.tensor_copy(
+                out=pick2[b][:, 1].rearrange("p (j s) -> p s j", j=4)[:, h * 64 : (h + 1) * 64, :],
+                in_=window(1).indirect(lists[b][:, h * 16 : (h + 1) * 16]),
             )
 
         def tv(b, u):
-            t = psum.tile([P, 4, P], F32, name="turned", bufs=4)
-            pairs = picked[b][:, u].rearrange("p n e -> p (n e)").bitcast(F32).rearrange("p (j s) -> p j s", j=4)
+            t = psum.tile([P, 4, P], F32, name="turned", tag=f"bank1{b}")
+            pairs = pick2[b][:, u].bitcast(F32).rearrange("p (j s) -> p j s", j=4)
             for j in range(4):
                 nc.tensor.transpose(t[:, j, :], pairs[:, j, :], ident_f[:])
             turned[b, u] = t
 
         def vc(b, u):
-            if (b, u) == (0, 0):
-                both = keep.tile([P, B, 2 * P, 4], BF16, name="vals_first", tag="raw4", align_bytes=64)
-                vals[0, 0], vals[1, 0] = both[:, 0], both[:, 1]
-            if (b, u) == (0, 1):
-                vals[b, u] = keep.tile([P, 2 * P, 4], BF16, name="vals01", align_bytes=64)[:]
-            if (b, u) == (1, 1):
-                vals[b, u] = keep.tile([P, 2 * P, 4], BF16, name="vals11", align_bytes=64)[:]
+            if u not in vals:
+                vals[u] = keep.tile([P, B * 1024], BF16, name="vals1", tag="pick1", align_bytes=64)
             nc.scalar.copy(
-                out=vals[b, u].rearrange("s (e p) j -> s e p j", e=2),
-                in_=turned[b, u][:].rearrange("s j p -> s (j p)").bitcast(BF16).rearrange("s (j p e) -> s e p j", j=4, e=2),
+                out=vals[u][:, b * 1024 : (b + 1) * 1024].rearrange("s (h e p j) -> s h e p j", h=H, e=2, j=4),
+                in_=turned[b, u][:]
+                .rearrange("s j p -> s (j p)")
+                .bitcast(BF16)
+                .rearrange("s (j h p e) -> s h e p j", j=4, h=H, e=2),
             )
 
         def qv(b, u):
             cols = slice(u * 2 * P, (u + 1) * 2 * P)
-            if "vq" not in vals:
-                vals["vq"] = keep.tile([P, B, DV], U32, name="vq", tag="trow1", align_bytes=64)
+            if "vq" not in late:
+                late["vq"] = keep.tile([P, B, DV], U32, name="vq", tag="raw4", align_bytes=64)
             nc.vector.quantize_mx(
-                out=vals["vq"][:, b, cols].bitcast(FP8X4),
+                out=late["vq"][:, b, cols].bitcast(FP8X4),
                 scales=vs[:, b, cols],
-                in_=vals[b, u].rearrange("p c j -> p (c j)"),
+                in_=vals[u][:, b * 1024 : (b + 1) * 1024],
             )
 
         def qc(b):
-            nc.scalar.activation(out=q_sb[:, b], in_=q_raw[b][:].rearrange("p t q -> p q t"), func=ACT.Copy)
+            nc.scalar.activation(out=q_sb[:, b], in_=q_raw[b].rearrange("p t q -> p q t"), func=ACT.Copy)
 
-        def qQ(b):
-            cols = slice(b * NQ, (b + 1) * NQ)
+        def qQ():
             nc.vector.quantize_mx(
-                out=qq[:, cols].bitcast(FP8X4), scales=qs[:, cols], in_=q_sb[:, b].rearrange("p q t -> p (q t)")
+                out=qq[:].bitcast(FP8X4), scales=qs[:], in_=q_sb[:].rearrange("p b q t -> p (b q t)")
             )
 
-        def ilv(b):
-            keys[b] = keep.tile([P, N, 2, 2], BF16, name=f"keys{b}", tag="keys", align_bytes=64)
-            copy, word = (nc.scalar.copy, U32) if b == 0 else (nc.vector.tensor_copy, I32)
-            copy(
-                out=keys[b][:].rearrange("p n u e -> p (n u e)").bitcast(word).rearrange("p (n u) -> p n u", u=2),
-                in_=picked[b][:].rearrange("p u n e -> p (u n e)").bitcast(word).rearrange("p (u n) -> p n u", u=2),
+        def ilv(b, h):
+            keys[b, h] = reuse.tile([P, N], U32, name=f"keys{b}{h}", align_bytes=64, offset=2048 * (b * H + h))[:]
+            nc.scalar.copy(
+                out=keys[b, h].rearrange("p (j s u) -> p j s u", j=4, u=2),
+                in_=pick2[b][:].rearrange("p u (j s) -> p j s u", j=4)[:, :, h * 64 : (h + 1) * 64, :],
             )
 
-        def qK(b):
+        def qK(b, h):
+            cols = slice(h * 2 * P, (h + 1) * 2 * P)
             nc.vector.quantize_mx(
-                out=kq[b][:].bitcast(FP8X4), scales=ks[b][:], in_=keys[b][:].rearrange("p n u e -> p (n u e)")
+                out=kq[b][:, cols].bitcast(FP8X4),
+                scales=ks[b][:, cols],
+                in_=keys[b, h].bitcast(BF16),
             )
 
-        def mm(b):
-            sc = psum.tile([P, N], F32, name="sc", tag="sc", bufs=2)
+        def mm(b, h):
+            cols = slice(h * 2 * P, (h + 1) * 2 * P)
+            sc = psum.tile([P, 2 * P], F32, name="sc", tag=f"acc{b}{h}")
             nc.tensor.matmul_mx(
                 out=sc[:],
                 lhsT=qq[:, b * NQ : (b + 1) * NQ].bitcast(FP8X4),
                 lhsT_scale=qs[:, b * NQ : (b + 1) * NQ],
-                rhs=kq[b][:].bitcast(FP8X4),
-                rhs_scale=ks[b][:],
+                rhs=kq[b][:, cols].bitcast(FP8X4),
+                rhs_scale=ks[b][:, cols],
                 start=True,
                 stop=True,
             )
-            scores[b] = sc
+            scores[b, h] = sc
 
-        def tok():
-            nc.vector.tensor_copy(out=toks[:].rearrange("p b n -> p (b n)"), in_=ts_sb[:].indirect(offsets[:]))
+        def tok(b):
+            nc.vector.tensor_copy(out=toks[b][:], in_=ts_sb[:].indirect(lists[b]))
 
         def tt(b):
-            t = psum.tile([P, 4, P], F32, name="tt", tag="pt", bufs=2)
+            t = psum.tile([P, 4, P], F32, name="tt", tag=f"bank0{b}")
             for j in range(4):
-                nc.tensor.transpose(t[:, j, :], toks[:, b, :].rearrange("q (s j) -> q j s", j=4)[:, j, :], ident_f[:])
+                nc.tensor.transpose(t[:, j, :], toks[b][:].rearrange("q (s j) -> q j s", j=4)[:, j, :], ident_f[:])
             tts[b] = t
 
         def tcl(b):
-            if b == 0:
-                both = keep.tile([P, B, 4], F32, name="tcols", tag="raw2", align_bytes=64)
-                tcol[0], tcol[1] = both[:, 0], both[:, 1]
-            nc.scalar.copy(out=tcol[b], in_=tts[b][:, :, 0])
+            nc.scalar.copy(out=tcol[b][:], in_=tts[b][:, :, 0])
 
-        def spread(b):
-            t = psum.tile([P, 4, P], F32, name="sp", tag="pt", bufs=2)
+        def spt(b):
+            t = psum.tile([P, 4, P], F32, name="sp", tag=f"bank0{b}")
             for j in range(4):
                 nc.tensor.transpose(t[:, j, :], tcol[b][:, j : j + 1].to_broadcast([P, P]), ident_f[:])
-            nc.scalar.copy(out=trow[b][:], in_=t[:].rearrange("q j s -> q (j s)"))
+            tts[b] = t
 
-        def sca(b):
-            a[b] = keep.tile([P, N], F32, name=f"a{b}", tag=f"a{b}", align_bytes=64)
-            nc.vector.tensor_tensor(out=a[b][:], in0=scores[b][:], in1=trow[b][:], op=ALU.mult)
+        def spc(b):
+            if "trow" not in late:
+                late["trow"] = keep.tile([P, B, 4, P], F32, name="trow", tag="raw4", align_bytes=64)
+            nc.scalar.copy(out=late["trow"][:, b], in_=tts[b][:])
+
+        def sca(b, h):
+            cols = slice(h * 64, (h + 1) * 64)
+            nc.vector.tensor_tensor(
+                out=a[b][:, :, cols],
+                in0=scores[b, h][:].rearrange("q (j s) -> q j s", j=4),
+                in1=late["trow"][:, b, :, cols],
+                op=ALU.mult,
+            )
 
         def mx(b):
             neg_m[b] = keep.tile([P, 1], F32, name=f"nm{b}")
             nc.vector.tensor_reduce(
                 out=neg_m[b][:],
-                in_=a[b][:],
+                in_=a[b][:].rearrange("q j s -> q (j s)"),
                 axis=mybir.AxisListType.X,
                 op=ALU.max,
                 negate=True,
             )
 
-        def ex(b):
-            p[b] = keep.tile([P, 4, P], F32, name=f"p{b}")
-            total[b] = keep.tile([P, 1], F32, name=f"total{b}")
+        def ex(b, h):
             nc.scalar.activation(
-                out=p[b][:].rearrange("q j s -> q (j s)"),
-                in_=a[b][:],
+                out=p[b][:, 2 * h : 2 * h + 2, :],
+                in_=a[b][:, 2 * h : 2 * h + 2, :],
                 func=ACT.Exp,
                 bias=neg_m[b][:],
                 scale=1.0,
-                accum_out=total[b][:],
+                accum_out=parts[:, b, h : h + 1],
             )
 
-        def pt(b):
-            t = psum.tile([P, 4, P], F32, name="pt", tag="pt", bufs=2)
-            for j in range(4):
-                nc.tensor.transpose(t[:, j, :], p[b][:, j, :], ident_f[:])
-            pts[b] = t
+        def pt(b, h):
+            if h == 0:
+                pts[b] = psum.tile([P, 4, P], F32, name="pt", tag=f"bank0{b}")
+            for j in range(2 * h, 2 * h + 2):
+                nc.tensor.transpose(pts[b][:, j, :], p[b][:, j, :], ident_f[:])
 
         def w(b):
             wts[b] = keep.tile([P, NQ, 4], BF16, name=f"w{b}", align_bytes=64)
             nc.vector.tensor_tensor(
                 out=wts[b][:],
                 in0=pts[b][:].rearrange("s j q -> s q j"),
-                in1=tcol[b].unsqueeze(1).to_broadcast([P, NQ, 4]),
+                in1=tcol[b][:].unsqueeze(1).to_broadcast([P, NQ, 4]),
                 op=ALU.mult,
             )
 
@@ -223,49 +242,54 @@ def tile_attend_mla_kernel(tc, qT, cT, ts, ch, offs, out):
             nc.vector.quantize_mx(out=wq[:].bitcast(FP8X4), scales=ws[:], in_=wts[b][:].rearrange("s q j -> s (q j)"))
             wqs[b] = (wq, ws)
 
-        def rec(b):
-            invs[b] = keep.tile([P, 1], F32, name=f"inv{b}")
-            nc.vector.reciprocal(out=invs[b][:], in_=total[b][:])
+        def rec():
+            nc.vector.tensor_reduce(out=total[:], in_=parts[:], axis=mybir.AxisListType.X, op=ALU.add)
+            nc.vector.reciprocal(out=inv[:], in_=total[:])
 
-        def mix(b):
+        def mix(b, h):
             wq, ws = wqs[b]
-            ys[b] = psum.tile([P, DV], F32, name="y", tag="sc", bufs=2)
-            nc.tensor.matmul_mx(
-                out=ys[b][:],
-                lhsT=wq[:].bitcast(FP8X4),
-                lhsT_scale=ws[:],
-                rhs=vals["vq"][:, b, :].bitcast(FP8X4),
-                rhs_scale=vs[:, b, :],
-                start=True,
-                stop=True,
-            )
+            ys[b, h] = psum.tile([P, 2 * P], F32, name="y", tag=f"acc{b}{h}")
+            for u in range(2):
+                cols = slice((2 * u + h) * P, (2 * u + h + 1) * P)
+                nc.tensor.matmul_mx(
+                    out=ys[b, h][:, u * P : (u + 1) * P],
+                    lhsT=wq[:].bitcast(FP8X4),
+                    lhsT_scale=ws[:],
+                    rhs=late["vq"][:, b, cols].bitcast(FP8X4),
+                    rhs_scale=vs[:, b, cols],
+                    start=True,
+                    stop=True,
+                )
 
-        def fin(b):
-            o = keep.tile([P, DV], F32, name=f"o{b}")
+        def fin(b, h):
+            cols = slice(h * 2 * P, (h + 1) * 2 * P)
+            o = keep.tile([P, 2 * P], F32, name=f"o{b}{h}")
             nc.vector.scalar_tensor_tensor(
                 out=o[:].rearrange("q (p f) -> q p f", f=4),
-                in0=ys[b][:].rearrange("q (f p) -> q p f", f=4),
-                scalar=invs[b][:],
-                in1=ch_sb[:].rearrange("q (p f) -> q p f", f=4),
+                in0=ys[b, h][:].rearrange("q (f p) -> q p f", f=4),
+                scalar=inv[:, b : b + 1],
+                in1=ch_sb[:, cols].rearrange("q (p f) -> q p f", f=4),
                 op0=ALU.mult,
                 op1=ALU.mult,
             )
-            nc.sync.dma_start(out=out[b], in_=o[:])
+            nc.sync.dma_start(out=out[b][:, cols], in_=o[:])
 
-        tok()
+        tok(0)
+        tok(1)
         cs(0)
         cs(1)
-        cv(2)
-        cs(2)
         tt(0)
         tt(1)
+        cv(2)
         cv(3)
         g(0, 0)
         tcl(0)
         tcl(1)
-        spread(0)
-        spread(1)
+        spt(0)
+        spt(1)
         cs(4)
+        spc(0)
+        spc(1)
         g(1, 0)
         tv(0, 0)
         vc(0, 0)
@@ -274,41 +298,57 @@ def tile_attend_mla_kernel(tc, qT, cT, ts, ch, offs, out):
         cv(6)
         vc(1, 0)
         cv(7)
-        g(0, 1)
+        gh(0, 0)
+        gh(0, 1)
+        gh(1, 0)
+        gh(1, 1)
         qc(0)
-        ilv(0)
-        g(1, 1)
-        qQ(0)
-        qK(0)
-        mm(0)
-        ilv(1)
         qc(1)
-        qQ(1)
-        qK(1)
-        mm(1)
+        ilv(0, 0)
+        ilv(0, 1)
+        ilv(1, 0)
+        ilv(1, 1)
+        qQ()
+        qK(0, 0)
+        mm(0, 0)
+        qK(0, 1)
+        mm(0, 1)
+        qK(1, 0)
+        mm(1, 0)
+        qK(1, 1)
+        mm(1, 1)
         tv(0, 1)
         tv(1, 1)
-        vc(0, 1)
-        sca(0)
+        sca(0, 0)
+        sca(0, 1)
         mx(0)
-        ex(0)
-        sca(1)
+        ex(0, 0)
+        pt(0, 0)
+        ex(0, 1)
+        pt(0, 1)
+        sca(1, 0)
+        sca(1, 1)
         mx(1)
-        ex(1)
+        ex(1, 0)
+        pt(1, 0)
+        ex(1, 1)
+        pt(1, 1)
+        vc(0, 1)
         vc(1, 1)
-        pt(0)
         w(0)
-        pt(1)
+        qw(0)
+        w(1)
+        qw(1)
         qv(0, 0)
         qv(0, 1)
-        qw(0)
-        mix(0)
-        w(1)
+        mix(0, 0)
+        mix(0, 1)
         qv(1, 0)
         qv(1, 1)
-        qw(1)
-        mix(1)
-        rec(0)
-        rec(1)
-        fin(0)
-        fin(1)
+        mix(1, 0)
+        mix(1, 1)
+        rec()
+        fin(0, 0)
+        fin(0, 1)
+        fin(1, 0)
+        fin(1, 1)

@@ -69,7 +69,7 @@ def tile_attend_mla_kernel(tc, qT, cT, ts, ch, offs, out):
         toks = [keep.tile([P, N], F32, name=f"toks{b}") for b in range(B)]
         tcol = [keep.tile([P, 4], F32, name=f"tcol{b}") for b in range(B)]
         vs = keep.tile([P, B, DV], U8, name="vs", align_bytes=64)
-        a = [keep.tile([P, 4, P], F32, name=f"a{b}") for b in range(B)]
+        a = [keep.tile([P, N], F32, name=f"a{b}") for b in range(B)]
         p = [keep.tile([P, 4, P], F32, name=f"p{b}") for b in range(B)]
         parts = keep.tile([P, B, H], F32, name="parts")
         total = keep.tile([P, B], F32, name="total")
@@ -94,19 +94,17 @@ def tile_attend_mla_kernel(tc, qT, cT, ts, ch, offs, out):
             return words[u][:].rearrange("p n e -> p (n e)").bitcast(U32)
 
         def g(b, u):
-            nc.vector.tensor_copy(
-                out=pick2[b][:, u].rearrange("p (j s) -> p s j", j=4), in_=window(u).indirect(lists[b])
-            )
+            nc.vector.tensor_copy(out=pick2[b][:, u], in_=window(u).indirect(lists[b]))
 
         def gh(b, h):
             nc.vector.tensor_copy(
-                out=pick2[b][:, 1].rearrange("p (j s) -> p s j", j=4)[:, h * 64 : (h + 1) * 64, :],
+                out=pick2[b][:, 1, h * 256 : (h + 1) * 256],
                 in_=window(1).indirect(lists[b][:, h * 16 : (h + 1) * 16]),
             )
 
         def tv(b, u):
             t = psum.tile([P, 4, P], F32, name="turned", tag=f"bank1{b}")
-            pairs = pick2[b][:, u].bitcast(F32).rearrange("p (j s) -> p j s", j=4)
+            pairs = pick2[b][:, u].bitcast(F32).rearrange("p (s j) -> p j s", j=4)
             for j in range(4):
                 nc.tensor.transpose(t[:, j, :], pairs[:, j, :], ident_f[:])
             turned[b, u] = t
@@ -143,8 +141,8 @@ def tile_attend_mla_kernel(tc, qT, cT, ts, ch, offs, out):
         def ilv(b, h):
             keys[b, h] = reuse.tile([P, N], U32, name=f"keys{b}{h}", align_bytes=64, offset=2048 * (b * H + h))[:]
             nc.scalar.copy(
-                out=keys[b, h].rearrange("p (j s u) -> p j s u", j=4, u=2),
-                in_=pick2[b][:].rearrange("p u (j s) -> p j s u", j=4)[:, :, h * 64 : (h + 1) * 64, :],
+                out=keys[b, h].rearrange("p (n u) -> p n u", u=2),
+                in_=pick2[b][:, :, h * 256 : (h + 1) * 256].rearrange("p u n -> p n u"),
             )
 
         def qK(b, h):
@@ -189,15 +187,17 @@ def tile_attend_mla_kernel(tc, qT, cT, ts, ch, offs, out):
 
         def spc(b):
             if "trow" not in late:
-                late["trow"] = keep.tile([P, B, 4, P], F32, name="trow", tag="raw4", align_bytes=64)
-            nc.scalar.copy(out=late["trow"][:, b], in_=tts[b][:])
+                late["trow"] = keep.tile([P, B, N], F32, name="trow", tag="raw4", align_bytes=64)
+            nc.scalar.copy(
+                out=late["trow"][:, b].rearrange("q (s j) -> q s j", j=4), in_=tts[b][:].rearrange("q j s -> q s j")
+            )
 
         def sca(b, h):
-            cols = slice(h * 64, (h + 1) * 64)
+            cols = slice(h * 256, (h + 1) * 256)
             nc.vector.tensor_tensor(
-                out=a[b][:, :, cols],
-                in0=scores[b, h][:].rearrange("q (j s) -> q j s", j=4),
-                in1=late["trow"][:, b, :, cols],
+                out=a[b][:, cols],
+                in0=scores[b, h][:],
+                in1=late["trow"][:, b, cols],
                 op=ALU.mult,
             )
 
@@ -205,7 +205,7 @@ def tile_attend_mla_kernel(tc, qT, cT, ts, ch, offs, out):
             neg_m[b] = keep.tile([P, 1], F32, name=f"nm{b}")
             nc.vector.tensor_reduce(
                 out=neg_m[b][:],
-                in_=a[b][:].rearrange("q j s -> q (j s)"),
+                in_=a[b][:],
                 axis=mybir.AxisListType.X,
                 op=ALU.max,
                 negate=True,
@@ -213,8 +213,8 @@ def tile_attend_mla_kernel(tc, qT, cT, ts, ch, offs, out):
 
         def ex(b, h):
             nc.scalar.activation(
-                out=p[b][:, 2 * h : 2 * h + 2, :],
-                in_=a[b][:, 2 * h : 2 * h + 2, :],
+                out=p[b][:, 2 * h : 2 * h + 2, :].rearrange("q j s -> q s j"),
+                in_=a[b][:].rearrange("q (s j) -> q s j", j=4)[:, :, 2 * h : 2 * h + 2],
                 func=ACT.Exp,
                 bias=neg_m[b][:],
                 scale=1.0,

@@ -19,7 +19,7 @@ FP8X4 = mybir.dt.float8_e4m3fn_x4
 ACT = mybir.ActivationFunctionType
 ALU = mybir.AluOpType
 
-CHUNKS = [(0, 0, 640, 0), (0, 640, 640, 0), (0, 1280, 512, 512), (0, 1792, 256, 256), (1, 0, 384, 0), (1, 384, 768, 768), (1, 1152, 640, 640), (1, 1792, 256, 256)]
+CHUNKS = [(0, 0, 768, 0), (0, 768, 768, 256), (0, 1536, 512, 512), (1, 0, 1024, 1024), (1, 1024, 768, 768), (1, 1792, 256, 256)]
 
 
 def tile_attend_mla_kernel(tc, qT, cT, ts, ch, offs, out):
@@ -41,7 +41,6 @@ def tile_attend_mla_kernel(tc, qT, cT, ts, ch, offs, out):
         make_identity(nc, ident_f[:])
 
         offsets = keep.tile([P, B * N // 16], U16, name="offsets")
-        nc.sync.dma_start(offsets[:], offs)
         lists = [offsets[:, b * (N // 16) : (b + 1) * (N // 16)] for b in range(B)]
         pool_rows = cT.rearrange("(p t) n -> p t n", t=PACK)
         raw = []
@@ -50,6 +49,7 @@ def tile_attend_mla_kernel(tc, qT, cT, ts, ch, offs, out):
             nc.sync.dma_start(out=r[:], in_=pool_rows[:, 2 * u : 2 * u + 2, c0 : c0 + w])
             raw.append(r)
             if i == 0:
+                nc.sync.dma_start(offsets[:], offs)
                 nc.sync.dma_start(out=ts_sb[0:1, :], in_=ts[0:1, :])
         q_both = reuse.tile([P, B * PACK * NQ], F32, name="q_both", offset=1024)
         q_raw = [q_both[:, b * PACK * NQ : (b + 1) * PACK * NQ].rearrange("p (t q) -> p t q", t=PACK) for b in range(B)]
@@ -67,14 +67,14 @@ def tile_attend_mla_kernel(tc, qT, cT, ts, ch, offs, out):
         qq = keep.tile([P, B * NQ], U32, name="qq", align_bytes=64)
         qs = keep.tile([P, B * NQ], U8, name="qs", align_bytes=64)
         toks = [keep.tile([P, N], F32, name=f"toks{b}") for b in range(B)]
-        tcol = [keep.tile([P, 4], F32, name=f"tcol{b}") for b in range(B)]
+        tcol = [keep.tile([P, 4], F32, name=f"tcol{b}", tag=f"tcol{b}", align_bytes=64) for b in range(B)]
         vs = keep.tile([P, B, DV], U8, name="vs", align_bytes=64)
         a = [keep.tile([P, N], F32, name=f"a{b}") for b in range(B)]
         p = [keep.tile([P, 4, P], F32, name=f"p{b}") for b in range(B)]
         parts = keep.tile([P, B, H], F32, name="parts")
         total = keep.tile([P, B], F32, name="total")
         inv = keep.tile([P, B], F32, name="inv")
-        turned, scores, tts, neg_m, pts, wts, wqs, ys, late, keys = ({} for i in range(10))
+        turned, scores, tts, neg_m, pts, wts, wqs, ys, late, keys, vq = ({} for i in range(11))
 
         def cv(i):
             u, c0, w, wv = CHUNKS[i]
@@ -121,14 +121,15 @@ def tile_attend_mla_kernel(tc, qT, cT, ts, ch, offs, out):
             )
 
         def qv(b, u):
-            cols = slice(u * 2 * P, (u + 1) * 2 * P)
-            if "vq" not in late:
-                late["vq"] = keep.tile([P, B, DV], U32, name="vq", tag="raw4", align_bytes=64)
-            nc.vector.quantize_mx(
-                out=late["vq"][:, b, cols].bitcast(FP8X4),
-                scales=vs[:, b, cols],
-                in_=vals[u][:, b * 1024 : (b + 1) * 1024],
-            )
+            if u == 0:
+                vq[b] = keep.tile([P, DV], U32, name=f"vq{b}", tag=("raw1", "tcol0")[b], align_bytes=64)
+            for h in range(H):
+                cols = slice((2 * h + u) * P, (2 * h + u + 1) * P)
+                nc.vector.quantize_mx(
+                    out=vq[b][:, cols].bitcast(FP8X4),
+                    scales=vs[:, b, cols],
+                    in_=vals[u][:, b * 1024 + h * 512 : b * 1024 + (h + 1) * 512],
+                )
 
         def qc(b):
             nc.scalar.activation(out=q_sb[:, b], in_=q_raw[b].rearrange("p t q -> p q t"), func=ACT.Copy)
@@ -187,7 +188,7 @@ def tile_attend_mla_kernel(tc, qT, cT, ts, ch, offs, out):
 
         def spc(b):
             if "trow" not in late:
-                late["trow"] = keep.tile([P, B, N], F32, name="trow", tag="raw4", align_bytes=64)
+                late["trow"] = keep.tile([P, B, N], F32, name="trow", tag="raw1", align_bytes=64)
             nc.scalar.copy(
                 out=late["trow"][:, b].rearrange("q (s j) -> q s j", j=4), in_=tts[b][:].rearrange("q j s -> q s j")
             )
@@ -228,7 +229,7 @@ def tile_attend_mla_kernel(tc, qT, cT, ts, ch, offs, out):
                 nc.tensor.transpose(pts[b][:, j, :], p[b][:, j, :], ident_f[:])
 
         def w(b):
-            wts[b] = keep.tile([P, NQ, 4], BF16, name=f"w{b}", align_bytes=64)
+            wts[b] = keep.tile([P, NQ, 4], BF16, name=f"w{b}", tag="w", align_bytes=64)
             nc.vector.tensor_tensor(
                 out=wts[b][:],
                 in0=pts[b][:].rearrange("s j q -> s q j"),
@@ -247,19 +248,18 @@ def tile_attend_mla_kernel(tc, qT, cT, ts, ch, offs, out):
             nc.vector.reciprocal(out=inv[:], in_=total[:])
 
         def mix(b, h):
+            cols = slice(h * 2 * P, (h + 1) * 2 * P)
             wq, ws = wqs[b]
             ys[b, h] = psum.tile([P, 2 * P], F32, name="y", tag=f"acc{b}{h}")
-            for u in range(2):
-                cols = slice((2 * u + h) * P, (2 * u + h + 1) * P)
-                nc.tensor.matmul_mx(
-                    out=ys[b, h][:, u * P : (u + 1) * P],
-                    lhsT=wq[:].bitcast(FP8X4),
-                    lhsT_scale=ws[:],
-                    rhs=late["vq"][:, b, cols].bitcast(FP8X4),
-                    rhs_scale=vs[:, b, cols],
-                    start=True,
-                    stop=True,
-                )
+            nc.tensor.matmul_mx(
+                out=ys[b, h][:],
+                lhsT=wq[:].bitcast(FP8X4),
+                lhsT_scale=ws[:],
+                rhs=vq[b][:, cols].bitcast(FP8X4),
+                rhs_scale=vs[:, b, cols],
+                start=True,
+                stop=True,
+            )
 
         def fin(b, h):
             cols = slice(h * 2 * P, (h + 1) * 2 * P)
@@ -278,26 +278,25 @@ def tile_attend_mla_kernel(tc, qT, cT, ts, ch, offs, out):
         tok(1)
         cs(0)
         cs(1)
+        cv(1)
         tt(0)
         tt(1)
         cv(2)
-        cv(3)
         g(0, 0)
         tcl(0)
         tcl(1)
         spt(0)
         spt(1)
-        cs(4)
+        g(1, 0)
+        cv(3)
         spc(0)
         spc(1)
-        g(1, 0)
         tv(0, 0)
         vc(0, 0)
         tv(1, 0)
-        cv(5)
-        cv(6)
+        cv(4)
         vc(1, 0)
-        cv(7)
+        cv(5)
         gh(0, 0)
         gh(0, 1)
         gh(1, 0)
@@ -335,19 +334,19 @@ def tile_attend_mla_kernel(tc, qT, cT, ts, ch, offs, out):
         pt(1, 1)
         vc(0, 1)
         vc(1, 1)
+        rec()
         w(0)
         qw(0)
-        w(1)
-        qw(1)
         qv(0, 0)
         qv(0, 1)
         mix(0, 0)
         mix(0, 1)
+        w(1)
+        qw(1)
         qv(1, 0)
         qv(1, 1)
         mix(1, 0)
         mix(1, 1)
-        rec()
         fin(0, 0)
         fin(0, 1)
         fin(1, 0)

@@ -19,7 +19,7 @@ FP8X4 = mybir.dt.float8_e4m3fn_x4
 ACT = mybir.ActivationFunctionType
 ALU = mybir.AluOpType
 
-CHUNKS = [(0, 0, 768, 0), (0, 768, 768, 256), (0, 1536, 512, 512), (1, 0, 1024, 1024), (1, 1024, 768, 768), (1, 1792, 256, 256)]
+CHUNKS = [(0, 0, 2048, 1376), (1, 0, 896, 0), (1, 896, 768, 768), (1, 1664, 384, 384)]
 
 
 def tile_attend_mla_kernel(tc, qT, cT, ts, ch, offs, out):
@@ -29,18 +29,20 @@ def tile_attend_mla_kernel(tc, qT, cT, ts, ch, offs, out):
         reuse = ctx.enter_context(tc.tile_pool(name="reuse", bufs=1))
         psum = ctx.enter_context(tc.psum_pool(name="psum", bufs=1))
 
+        ts_sb = keep.tile([P, T], F32, name="ts_sb")
         warm = keep.tile([P, 1], F32, name="warm")
         nc.vector.memset(warm[:], 0.0)
         warm2 = keep.tile([P, 1], F32, name="warm2")
         nc.scalar.activation(out=warm2[:], in_=warm[:], func=ACT.Exp)
-        ts_sb = keep.tile([P, T], F32, name="ts_sb")
-        nc.gpsimd.memset(ts_sb[:, T // 2 : T], 0.0)
-        nc.vector.memset(ts_sb[:, 0 : T // 2 - 1], 0.0)
-        nc.vector.memset(ts_sb[:, T // 2 - 1 : T // 2], 0.0)
+        nc.gpsimd.memset(ts_sb[0 : P - 1, 1536:T], 0.0)
+        nc.vector.memset(ts_sb[0 : P - 1, 0:1535], 0.0)
+        nc.vector.memset(ts_sb[0 : P - 1, 1535:1536], 0.0)
         ident_f = keep.tile([P, P], F32, name="ident_f")
         make_identity(nc, ident_f[:])
 
         offsets = keep.tile([P, B * N // 16], U16, name="offsets")
+        nc.sync.dma_start(offsets[:], offs)
+        nc.sync.dma_start(out=ts_sb[P - 1 : P, :], in_=ts[0:1, :])
         lists = [offsets[:, b * (N // 16) : (b + 1) * (N // 16)] for b in range(B)]
         pool_rows = cT.rearrange("(p t) n -> p t n", t=PACK)
         raw = []
@@ -48,22 +50,19 @@ def tile_attend_mla_kernel(tc, qT, cT, ts, ch, offs, out):
             r = keep.tile([P, 2, w], F32, name=f"raw{i}", tag=f"raw{i}", align_bytes=64)
             nc.sync.dma_start(out=r[:], in_=pool_rows[:, 2 * u : 2 * u + 2, c0 : c0 + w])
             raw.append(r)
-            if i == 0:
-                nc.sync.dma_start(offsets[:], offs)
-                nc.sync.dma_start(out=ts_sb[0:1, :], in_=ts[0:1, :])
-        q_both = reuse.tile([P, B * PACK * NQ], F32, name="q_both", offset=1024)
-        q_raw = [q_both[:, b * PACK * NQ : (b + 1) * PACK * NQ].rearrange("p (t q) -> p t q", t=PACK) for b in range(B)]
+        q_raw = [keep.tile([P, PACK, NQ], F32, name=f"q_raw{b}", tag=f"q_raw{b}", align_bytes=64) for b in range(B)]
         for b in range(B):
-            nc.sync.dma_start(out=q_raw[b], in_=qT[b].rearrange("(p t) q -> p t q", t=PACK))
+            nc.sync.dma_start(out=q_raw[b][:], in_=qT[b].rearrange("(p t) q -> p t q", t=PACK))
         ch_sb = keep.tile([P, DV], F32, name="ch_sb")
         nc.sync.dma_start(out=ch_sb[:], in_=ch)
 
         words = [keep.tile([P, T, 2], BF16, name=f"words{u}") for u in range(2)]
         pick2 = [keep.tile([P, 2, N], U32, name=f"pick{b}", tag=f"pick{b}", align_bytes=64) for b in range(B)]
-        kq = [keep.tile([P, N], U32, name=f"kq{b}", align_bytes=64) for b in range(B)]
+        kq = {}
         ks = [keep.tile([P, N], U8, name=f"ks{b}", align_bytes=64) for b in range(B)]
-        vals = {0: keep.tile([P, B * 1024], BF16, name="vals0", align_bytes=64)}
-        q_sb = reuse.tile([P, B, NQ, PACK], BF16, name="q_sb", align_bytes=64, offset=6144)
+        early = keep.tile([P, 2, 512], BF16, name="early", tag="raw1", align_bytes=64)
+        vals = {(0, 0, 0): early[:, 0], (0, 0, 1): early[:, 1]}
+        q_sb = [keep.tile([P, NQ, PACK], BF16, name=f"q_sb{b}", align_bytes=64) for b in range(B)]
         qq = keep.tile([P, B * NQ], U32, name="qq", align_bytes=64)
         qs = keep.tile([P, B * NQ], U8, name="qs", align_bytes=64)
         toks = [keep.tile([P, N], F32, name=f"toks{b}") for b in range(B)]
@@ -103,40 +102,51 @@ def tile_attend_mla_kernel(tc, qT, cT, ts, ch, offs, out):
             )
 
         def tv(b, u):
-            t = psum.tile([P, 4, P], F32, name="turned", tag=f"bank1{b}")
+            t = psum.tile([P, 4, P], F32, name="turned", tag="bank01" if (b, u) == (1, 1) else f"bank1{b}")
             pairs = pick2[b][:, u].bitcast(F32).rearrange("p (s j) -> p j s", j=4)
             for j in range(4):
                 nc.tensor.transpose(t[:, j, :], pairs[:, j, :], ident_f[:])
             turned[b, u] = t
 
-        def vc(b, u):
-            if u not in vals:
-                vals[u] = keep.tile([P, B * 1024], BF16, name="vals1", tag="pick1", align_bytes=64)
+        def vc(b, u, h):
+            if (b, u, h) not in vals:
+                rest = keep.tile([P, 6, 512], BF16, name="rest", tag="pick1", align_bytes=64)
+                for i, key in enumerate([(1, 0, 0), (1, 0, 1), (0, 1, 0), (0, 1, 1), (1, 1, 0), (1, 1, 1)]):
+                    vals[key] = rest[:, i]
             nc.scalar.copy(
-                out=vals[u][:, b * 1024 : (b + 1) * 1024].rearrange("s (h e p j) -> s h e p j", h=H, e=2, j=4),
+                out=vals[b, u, h].rearrange("s (e p j) -> s e p j", e=2, j=4),
                 in_=turned[b, u][:]
                 .rearrange("s j p -> s (j p)")
                 .bitcast(BF16)
-                .rearrange("s (j h p e) -> s h e p j", j=4, h=H, e=2),
+                .rearrange("s (j h p e) -> s h e p j", j=4, h=H, e=2)[:, h],
             )
 
         def qv(b, u):
             if u == 0:
-                vq[b] = keep.tile([P, DV], U32, name=f"vq{b}", tag=("raw1", "tcol0")[b], align_bytes=64)
+                vq[b] = keep.tile([P, DV], U32, name=f"vq{b}", tag=("trow", "tcol0")[b], align_bytes=64)
             for h in range(H):
                 cols = slice((2 * h + u) * P, (2 * h + u + 1) * P)
                 nc.vector.quantize_mx(
                     out=vq[b][:, cols].bitcast(FP8X4),
                     scales=vs[:, b, cols],
-                    in_=vals[u][:, b * 1024 + h * 512 : b * 1024 + (h + 1) * 512],
+                    in_=vals[b, u, h],
                 )
 
         def qc(b):
-            nc.scalar.activation(out=q_sb[:, b], in_=q_raw[b].rearrange("p t q -> p q t"), func=ACT.Copy)
+            nc.gpsimd.tensor_scalar(
+                out=q_sb[b][:],
+                in0=q_raw[b][:].rearrange("p t q -> p q t"),
+                scalar1=1.0,
+                scalar2=0.0,
+                op0=ALU.mult,
+                op1=ALU.add,
+            )
 
-        def qQ():
+        def qQ(b):
             nc.vector.quantize_mx(
-                out=qq[:].bitcast(FP8X4), scales=qs[:], in_=q_sb[:].rearrange("p b q t -> p (b q t)")
+                out=qq[:, b * NQ : (b + 1) * NQ].bitcast(FP8X4),
+                scales=qs[:, b * NQ : (b + 1) * NQ],
+                in_=q_sb[b][:].rearrange("p q t -> p (q t)"),
             )
 
         def ilv(b, h):
@@ -148,6 +158,8 @@ def tile_attend_mla_kernel(tc, qT, cT, ts, ch, offs, out):
 
         def qK(b, h):
             cols = slice(h * 2 * P, (h + 1) * 2 * P)
+            if h == 0:
+                kq[b] = keep.tile([P, N], U32, name=f"kq{b}", tag=f"q_raw{b}", align_bytes=64)
             nc.vector.quantize_mx(
                 out=kq[b][:, cols].bitcast(FP8X4),
                 scales=ks[b][:, cols],
@@ -169,26 +181,29 @@ def tile_attend_mla_kernel(tc, qT, cT, ts, ch, offs, out):
             scores[b, h] = sc
 
         def tok(b):
-            nc.vector.tensor_copy(out=toks[b][:], in_=ts_sb[:].indirect(lists[b]))
+            nc.vector.tensor_copy(
+                out=toks[b][:].bitcast(U32).rearrange("q (j s) -> q s j", j=4),
+                in_=ts_sb[:].bitcast(U32).indirect(lists[b]),
+            )
 
         def tt(b):
-            t = psum.tile([P, 4, P], F32, name="tt", tag=f"bank0{b}")
+            t = psum.tile([P, 4, P], F32, name="tt", tag="bank00")
             for j in range(4):
-                nc.tensor.transpose(t[:, j, :], toks[b][:].rearrange("q (s j) -> q j s", j=4)[:, j, :], ident_f[:])
+                nc.tensor.transpose(t[:, j, :], toks[b][:, j * P : (j + 1) * P], ident_f[:])
             tts[b] = t
 
         def tcl(b):
-            nc.scalar.copy(out=tcol[b][:], in_=tts[b][:, :, 0])
+            nc.scalar.copy(out=tcol[b][:], in_=tts[b][:, :, P - 1])
 
         def spt(b):
-            t = psum.tile([P, 4, P], F32, name="sp", tag=f"bank0{b}")
+            t = psum.tile([P, 4, P], F32, name="sp", tag=f"acc{b}0")
             for j in range(4):
                 nc.tensor.transpose(t[:, j, :], tcol[b][:, j : j + 1].to_broadcast([P, P]), ident_f[:])
             tts[b] = t
 
         def spc(b):
             if "trow" not in late:
-                late["trow"] = keep.tile([P, B, N], F32, name="trow", tag="raw1", align_bytes=64)
+                late["trow"] = keep.tile([P, B, N], F32, name="trow", tag="trow", align_bytes=64)
             nc.scalar.copy(
                 out=late["trow"][:, b].rearrange("q (s j) -> q s j", j=4), in_=tts[b][:].rearrange("q j s -> q s j")
             )
@@ -224,7 +239,7 @@ def tile_attend_mla_kernel(tc, qT, cT, ts, ch, offs, out):
 
         def pt(b, h):
             if h == 0:
-                pts[b] = psum.tile([P, 4, P], F32, name="pt", tag=f"bank0{b}")
+                pts[b] = psum.tile([P, 4, P], F32, name="pt", tag=("bank00", "bank11")[b])
             for j in range(2 * h, 2 * h + 2):
                 nc.tensor.transpose(pts[b][:, j, :], p[b][:, j, :], ident_f[:])
 
@@ -261,12 +276,12 @@ def tile_attend_mla_kernel(tc, qT, cT, ts, ch, offs, out):
                 stop=True,
             )
 
-        def fin(b, h):
-            cols = slice(h * 2 * P, (h + 1) * 2 * P)
-            o = keep.tile([P, 2 * P], F32, name=f"o{b}{h}")
+        def fin(b, h, first, count):
+            cols = slice(h * 2 * P + 4 * first, h * 2 * P + 4 * (first + count))
+            o = keep.tile([P, 4 * count], F32, name=f"o{b}{h}{first}")
             nc.vector.scalar_tensor_tensor(
                 out=o[:].rearrange("q (p f) -> q p f", f=4),
-                in0=ys[b, h][:].rearrange("q (f p) -> q p f", f=4),
+                in0=ys[b, h][:].rearrange("q (f p) -> q p f", f=4)[:, first : first + count, :],
                 scalar=inv[:, b : b + 1],
                 in1=ch_sb[:, cols].rearrange("q (p f) -> q p f", f=4),
                 op0=ALU.mult,
@@ -276,27 +291,25 @@ def tile_attend_mla_kernel(tc, qT, cT, ts, ch, offs, out):
 
         tok(0)
         tok(1)
-        cs(0)
-        cs(1)
-        cv(1)
         tt(0)
-        tt(1)
-        cv(2)
-        g(0, 0)
         tcl(0)
-        tcl(1)
         spt(0)
-        spt(1)
-        g(1, 0)
-        cv(3)
         spc(0)
+        tt(1)
+        cv(0)
+        cs(0)
+        tcl(1)
+        spt(1)
         spc(1)
+        g(0, 0)
+        g(1, 0)
+        cs(1)
         tv(0, 0)
-        vc(0, 0)
+        vc(0, 0, 0)
+        vc(0, 0, 1)
         tv(1, 0)
-        cv(4)
-        vc(1, 0)
-        cv(5)
+        cv(2)
+        cv(3)
         gh(0, 0)
         gh(0, 1)
         gh(1, 0)
@@ -307,11 +320,12 @@ def tile_attend_mla_kernel(tc, qT, cT, ts, ch, offs, out):
         ilv(0, 1)
         ilv(1, 0)
         ilv(1, 1)
-        qQ()
+        qQ(0)
         qK(0, 0)
         mm(0, 0)
         qK(0, 1)
         mm(0, 1)
+        qQ(1)
         qK(1, 0)
         mm(1, 0)
         qK(1, 1)
@@ -332,8 +346,12 @@ def tile_attend_mla_kernel(tc, qT, cT, ts, ch, offs, out):
         pt(1, 0)
         ex(1, 1)
         pt(1, 1)
-        vc(0, 1)
-        vc(1, 1)
+        vc(0, 1, 0)
+        vc(0, 1, 1)
+        vc(1, 0, 0)
+        vc(1, 0, 1)
+        vc(1, 1, 0)
+        vc(1, 1, 1)
         rec()
         w(0)
         qw(0)
@@ -347,7 +365,8 @@ def tile_attend_mla_kernel(tc, qT, cT, ts, ch, offs, out):
         qv(1, 1)
         mix(1, 0)
         mix(1, 1)
-        fin(0, 0)
-        fin(0, 1)
-        fin(1, 0)
-        fin(1, 1)
+        fin(0, 0, 0, 64)
+        fin(0, 1, 0, 64)
+        fin(1, 0, 0, 64)
+        fin(1, 1, 0, 32)
+        fin(1, 1, 32, 32)

@@ -30,10 +30,6 @@ def tile_attend_mla_kernel(tc, qT, cT, ts, ch, offs, out):
         psum = ctx.enter_context(tc.psum_pool(name="psum", bufs=1))
 
         ts_sb = keep.tile([P, T], F32, name="ts_sb")
-        warm = keep.tile([P, 1], F32, name="warm")
-        nc.vector.memset(warm[:], 0.0)
-        warm2 = keep.tile([P, 1], F32, name="warm2")
-        nc.scalar.activation(out=warm2[:], in_=warm[:], func=ACT.Exp)
         nc.gpsimd.memset(ts_sb[0 : P - 1, 1536:T], 0.0)
         nc.vector.memset(ts_sb[0 : P - 1, 0:1535], 0.0)
         nc.vector.memset(ts_sb[0 : P - 1, 1535:1536], 0.0)

@@ -6,227 +6,217 @@ from concourse.masks import make_identity
 B, N, T, D, DV, NQ = 2, 512, 2048, 512, 512, 128
 P = 128
 PACK = 4
-H = 2
+HALF = N // 2
 FLOPS = 2 * B * NQ * N * (D + DV)
 
 F32 = mybir.dt.float32
 BF16 = mybir.dt.bfloat16
 U32 = mybir.dt.uint32
-I32 = mybir.dt.int32
 U16 = mybir.dt.uint16
 U8 = mybir.dt.uint8
 FP8X4 = mybir.dt.float8_e4m3fn_x4
 ACT = mybir.ActivationFunctionType
 ALU = mybir.AluOpType
 
-CHUNKS = [(0, 0, 2048, 1376), (1, 0, 896, 0), (1, 896, 768, 768), (1, 1664, 384, 384)]
+HEAD = 512
+KB = 1024
+PLANE_AT = [8 * KB * t for t in range(PACK)]
+QRAW_AT = [32 * KB + 2 * KB * b for b in range(B)]
+TOKS_AT = [44 * KB + 2 * KB * b for b in range(B)]
+SPARE_AT = 48 * KB
+LIES_ON = {
+    "picked10": TOKS_AT[0],
+    "tcol1": PLANE_AT[0],
+    "q_sb1": PLANE_AT[3] + KB,
+    "vals": QRAW_AT[1] + KB,
+    "kq1": QRAW_AT[0],
+    "trow1": SPARE_AT + KB,
+    "vq0": SPARE_AT,
+    "vq1": SPARE_AT + 2 * KB,
+}
 
 
 def tile_attend_mla_kernel(tc, qT, cT, ts, ch, offs, out):
     nc = tc.nc
     with ExitStack() as ctx:
         keep = ctx.enter_context(tc.tile_pool(name="keep", bufs=1))
-        reuse = ctx.enter_context(tc.tile_pool(name="reuse", bufs=1))
+        over = ctx.enter_context(tc.tile_pool(name="over", bufs=1))
         psum = ctx.enter_context(tc.psum_pool(name="psum", bufs=1))
 
         ts_sb = keep.tile([P, T], F32, name="ts_sb")
         nc.gpsimd.memset(ts_sb[0 : P - 1, 1536:T], 0.0)
         nc.vector.memset(ts_sb[0 : P - 1, 0:1535], 0.0)
         nc.vector.memset(ts_sb[0 : P - 1, 1535:1536], 0.0)
-        ident_f = keep.tile([P, P], F32, name="ident_f")
-        make_identity(nc, ident_f[:])
+        ident = keep.tile([P, P], F32, name="ident")
+        make_identity(nc, ident[:])
 
         offsets = keep.tile([P, B * N // 16], U16, name="offsets")
         nc.sync.dma_start(offsets[:], offs)
         nc.sync.dma_start(out=ts_sb[P - 1 : P, :], in_=ts[0:1, :])
-        lists = [offsets[:, b * (N // 16) : (b + 1) * (N // 16)] for b in range(B)]
         pool_rows = cT.rearrange("(p t) n -> p t n", t=PACK)
-        raw = []
-        for i, (u, c0, w, wv) in enumerate(CHUNKS):
-            r = keep.tile([P, 2, w], F32, name=f"raw{i}", tag=f"raw{i}", align_bytes=64)
-            nc.sync.dma_start(out=r[:], in_=pool_rows[:, 2 * u : 2 * u + 2, c0 : c0 + w])
-            raw.append(r)
-        q_raw = [keep.tile([P, PACK, NQ], F32, name=f"q_raw{b}", tag=f"q_raw{b}", align_bytes=64) for b in range(B)]
+        planes = [over.tile([P, T], F32, name=f"plane{t}", align_bytes=64, offset=PLANE_AT[t]) for t in range(PACK)]
+        nc.scalar.dma_start(out=planes[0][:, :HEAD], in_=pool_rows[:, 0, :HEAD])
+        nc.sync.dma_start(out=planes[0][:, HEAD:], in_=pool_rows[:, 0, HEAD:])
+        for t in range(1, PACK):
+            nc.sync.dma_start(out=planes[t][:], in_=pool_rows[:, t, :])
+        q_raw = [over.tile([P, PACK, NQ], F32, name=f"q_raw{b}", align_bytes=64, offset=QRAW_AT[b]) for b in range(B)]
         for b in range(B):
             nc.sync.dma_start(out=q_raw[b][:], in_=qT[b].rearrange("(p t) q -> p t q", t=PACK))
         ch_sb = keep.tile([P, DV], F32, name="ch_sb")
         nc.sync.dma_start(out=ch_sb[:], in_=ch)
 
-        words = [keep.tile([P, T, 2], BF16, name=f"words{u}") for u in range(2)]
-        pick2 = [keep.tile([P, 2, N], U32, name=f"pick{b}", tag=f"pick{b}", align_bytes=64) for b in range(B)]
-        kq = {}
         ks = [keep.tile([P, N], U8, name=f"ks{b}", align_bytes=64) for b in range(B)]
-        early = keep.tile([P, 2, 512], BF16, name="early", tag="raw1", align_bytes=64)
-        vals = {(0, 0, 0): early[:, 0], (0, 0, 1): early[:, 1]}
-        q_sb = [keep.tile([P, NQ, PACK], BF16, name=f"q_sb{b}", align_bytes=64) for b in range(B)]
-        qq = keep.tile([P, B * NQ], U32, name="qq", align_bytes=64)
-        qs = keep.tile([P, B * NQ], U8, name="qs", align_bytes=64)
-        toks = [keep.tile([P, N], F32, name=f"toks{b}") for b in range(B)]
-        tcol = [keep.tile([P, 4], F32, name=f"tcol{b}", tag=f"tcol{b}", align_bytes=64) for b in range(B)]
-        vs = keep.tile([P, B, DV], U8, name="vs", align_bytes=64)
+        vs = [keep.tile([P, DV], U8, name=f"vs{b}", align_bytes=64) for b in range(B)]
+        qq = [keep.tile([P, NQ], U32, name=f"qq{b}", align_bytes=64) for b in range(B)]
+        qs = [keep.tile([P, NQ], U8, name=f"qs{b}", align_bytes=64) for b in range(B)]
+        toks = [over.tile([P, N], F32, name=f"toks{b}", align_bytes=64, offset=TOKS_AT[b]) for b in range(B)]
         a = [keep.tile([P, N], F32, name=f"a{b}") for b in range(B)]
-        p = [keep.tile([P, 4, P], F32, name=f"p{b}") for b in range(B)]
-        parts = keep.tile([P, B, H], F32, name="parts")
+        p = [keep.tile([P, PACK, P], F32, name=f"p{b}") for b in range(B)]
+        neg_m = [keep.tile([P, 1], F32, name=f"neg_m{b}") for b in range(B)]
+        parts = keep.tile([P, B, 2], F32, name="parts")
         total = keep.tile([P, B], F32, name="total")
         inv = keep.tile([P, B], F32, name="inv")
-        turned, scores, tts, neg_m, pts, wts, wqs, ys, late, keys, vq = ({} for i in range(11))
+        wts = [keep.tile([P, NQ, PACK], BF16, name=f"w{b}", align_bytes=64) for b in range(B)]
+        wq = [keep.tile([P, NQ], U32, name=f"wq{b}", align_bytes=64) for b in range(B)]
+        ws = [keep.tile([P, NQ], U8, name=f"ws{b}", align_bytes=64) for b in range(B)]
+        turned, scores, tts, pts, ys, made = ({} for i in range(6))
 
-        def cv(i):
-            u, c0, w, wv = CHUNKS[i]
+        def late(name, width, dt):
+            if name not in made:
+                if name in LIES_ON:
+                    made[name] = over.tile([P, width], dt, name=name, align_bytes=64, offset=LIES_ON[name])
+                else:
+                    made[name] = keep.tile([P, width], dt, name=name, align_bytes=64)
+            return made[name]
+
+        def tcol(b):
+            return late(f"tcol{b}", PACK, F32)
+
+        def trow(b):
+            return late(f"trow{b}", N, F32)
+
+        def picked(b, u):
+            return late(f"picked{b}{u}", 2 * N, BF16)
+
+        def keys(b):
+            return late(f"keys{b}", N * PACK, BF16)
+
+        def vals():
+            return late("vals", B * DV * PACK, BF16)
+
+        def vq(b):
+            return late(f"vq{b}", DV, U32)
+
+        def kq(b):
+            return late(f"kq{b}", N, U32)
+
+        def q_sb(b):
+            return late(f"q_sb{b}", NQ * PACK, BF16)
+
+        def entries(b, first, count):
+            col = (b * N + first) // 16
+            return offsets[:, col : col + count // 16]
+
+        def gather(b, t, first, count, on_scalar):
+            at = (t % 2) * N + first
+            dst = picked(b, t // 2)[:, at : at + count]
+            src = planes[t][:].indirect(entries(b, first, count))
+            if on_scalar:
+                nc.scalar.activation(out=dst, in_=src, func=ACT.Copy)
+            else:
+                nc.vector.tensor_copy(out=dst, in_=src)
+
+        def weave(b, u, first, count):
             nc.vector.tensor_copy(
-                out=words[u][:, c0 : c0 + wv, :], in_=raw[i][:, :, 0:wv].rearrange("p e n -> p n e")
+                out=keys(b)[:].rearrange("p (n t) -> p n t", t=PACK)[:, first : first + count, 2 * u : 2 * u + 2],
+                in_=picked(b, u)[:].rearrange("p (e n) -> p n e", e=2)[:, first : first + count, :],
             )
 
-        def cs(i):
-            u, c0, w, wv = CHUNKS[i]
-            nc.scalar.activation(
-                out=words[u][:, c0 + wv : c0 + w, :],
-                in_=raw[i][:, :, wv:w].rearrange("p e n -> p n e"),
-                func=ACT.Copy,
-            )
+        def tv(b, t):
+            if b == 0:
+                turned[t] = psum.tile([P, B, 2, P], F32, name="turned", tag=f"turn{t}")
+            words = picked(b, t // 2)[:, (t % 2) * N : (t % 2 + 1) * N].bitcast(F32).rearrange("p (s u) -> p u s", u=2)
+            for u in range(2):
+                nc.tensor.transpose(turned[t][:, b, u, :], words[:, u, :], ident[:])
 
-        def window(u):
-            return words[u][:].rearrange("p n e -> p (n e)").bitcast(U32)
-
-        def g(b, u):
-            nc.vector.tensor_copy(out=pick2[b][:, u], in_=window(u).indirect(lists[b]))
-
-        def gh(b, h):
-            nc.vector.tensor_copy(
-                out=pick2[b][:, 1, h * 256 : (h + 1) * 256],
-                in_=window(1).indirect(lists[b][:, h * 16 : (h + 1) * 16]),
-            )
-
-        def tv(b, u):
-            t = psum.tile([P, 4, P], F32, name="turned", tag="bank01" if (b, u) == (1, 1) else f"bank1{b}")
-            pairs = pick2[b][:, u].bitcast(F32).rearrange("p (s j) -> p j s", j=4)
-            for j in range(4):
-                nc.tensor.transpose(t[:, j, :], pairs[:, j, :], ident_f[:])
-            turned[b, u] = t
-
-        def vc(b, u, h):
-            if (b, u, h) not in vals:
-                rest = keep.tile([P, 6, 512], BF16, name="rest", tag="pick1", align_bytes=64)
-                for i, key in enumerate([(1, 0, 0), (1, 0, 1), (0, 1, 0), (0, 1, 1), (1, 1, 0), (1, 1, 1)]):
-                    vals[key] = rest[:, i]
+        def vc(t):
             nc.scalar.copy(
-                out=vals[b, u, h].rearrange("s (e p j) -> s e p j", e=2, j=4),
-                in_=turned[b, u][:]
-                .rearrange("s j p -> s (j p)")
-                .bitcast(BF16)
-                .rearrange("s (j h p e) -> s h e p j", j=4, h=H, e=2)[:, h],
+                out=vals()[:].bitcast(F32).rearrange("s (b h t p u) -> s t b h p u", b=B, h=2, t=PACK, u=2)[:, t],
+                in_=turned[t][:].rearrange("s b u (h p) -> s b h p u", h=2),
             )
 
-        def qv(b, u):
-            if u == 0:
-                vq[b] = keep.tile([P, DV], U32, name=f"vq{b}", tag=("trow", "tcol0")[b], align_bytes=64)
-            for h in range(H):
-                cols = slice((2 * h + u) * P, (2 * h + u + 1) * P)
-                nc.vector.quantize_mx(
-                    out=vq[b][:, cols].bitcast(FP8X4),
-                    scales=vs[:, b, cols],
-                    in_=vals[b, u, h],
-                )
+        def qv(b, h):
+            cols = slice(h * 2 * P, (h + 1) * 2 * P)
+            at = (2 * b + h) * 2 * P * PACK
+            nc.vector.quantize_mx(
+                out=vq(b)[:, cols].bitcast(FP8X4), scales=vs[b][:, cols], in_=vals()[:, at : at + 2 * P * PACK]
+            )
 
         def qc(b):
-            nc.gpsimd.tensor_scalar(
-                out=q_sb[b][:],
-                in0=q_raw[b][:].rearrange("p t q -> p q t"),
-                scalar1=1.0,
-                scalar2=0.0,
-                op0=ALU.mult,
-                op1=ALU.add,
+            nc.scalar.copy(
+                out=q_sb(b)[:].rearrange("p (c i t) -> p c t i", i=4, t=PACK),
+                in_=q_raw[b][:].rearrange("p t (c i) -> p c t i", i=4),
             )
 
         def qQ(b):
-            nc.vector.quantize_mx(
-                out=qq[:, b * NQ : (b + 1) * NQ].bitcast(FP8X4),
-                scales=qs[:, b * NQ : (b + 1) * NQ],
-                in_=q_sb[b][:].rearrange("p q t -> p (q t)"),
-            )
+            nc.vector.quantize_mx(out=qq[b][:].bitcast(FP8X4), scales=qs[b][:], in_=q_sb(b)[:])
 
-        def ilv(b, h):
-            keys[b, h] = reuse.tile([P, N], U32, name=f"keys{b}{h}", align_bytes=64, offset=2048 * (b * H + h))[:]
-            nc.scalar.copy(
-                out=keys[b, h].rearrange("p (n u) -> p n u", u=2),
-                in_=pick2[b][:, :, h * 256 : (h + 1) * 256].rearrange("p u n -> p n u"),
-            )
-
-        def qK(b, h):
-            cols = slice(h * 2 * P, (h + 1) * 2 * P)
-            if h == 0:
-                kq[b] = keep.tile([P, N], U32, name=f"kq{b}", tag=f"q_raw{b}", align_bytes=64)
+        def qK(b, first, count):
+            cols = slice(first, first + count)
             nc.vector.quantize_mx(
-                out=kq[b][:, cols].bitcast(FP8X4),
+                out=kq(b)[:, cols].bitcast(FP8X4),
                 scales=ks[b][:, cols],
-                in_=keys[b, h].bitcast(BF16),
+                in_=keys(b)[:, PACK * first : PACK * (first + count)],
             )
 
         def mm(b, h):
-            cols = slice(h * 2 * P, (h + 1) * 2 * P)
-            sc = psum.tile([P, 2 * P], F32, name="sc", tag=f"acc{b}{h}")
+            cols = slice(h * HALF, (h + 1) * HALF)
+            scores[b, h] = psum.tile([P, HALF], F32, name="scores", tag=f"acc{b}{h}")
             nc.tensor.matmul_mx(
-                out=sc[:],
-                lhsT=qq[:, b * NQ : (b + 1) * NQ].bitcast(FP8X4),
-                lhsT_scale=qs[:, b * NQ : (b + 1) * NQ],
-                rhs=kq[b][:, cols].bitcast(FP8X4),
+                out=scores[b, h][:],
+                lhsT=qq[b][:].bitcast(FP8X4),
+                lhsT_scale=qs[b][:],
+                rhs=kq(b)[:, cols].bitcast(FP8X4),
                 rhs_scale=ks[b][:, cols],
                 start=True,
                 stop=True,
             )
-            scores[b, h] = sc
 
         def tok(b):
             nc.vector.tensor_copy(
-                out=toks[b][:].bitcast(U32).rearrange("q (j s) -> q s j", j=4),
-                in_=ts_sb[:].bitcast(U32).indirect(lists[b]),
+                out=toks[b][:].bitcast(U32).rearrange("q (j s) -> q s j", j=PACK),
+                in_=ts_sb[:].bitcast(U32).indirect(entries(b, 0, N)),
             )
 
         def tt(b):
-            t = psum.tile([P, 4, P], F32, name="tt", tag="bank00")
-            for j in range(4):
-                nc.tensor.transpose(t[:, j, :], toks[b][:, j * P : (j + 1) * P], ident_f[:])
-            tts[b] = t
+            tts[b] = psum.tile([P, PACK, P], F32, name="tt", tag=f"turn{b}")
+            for j in range(PACK):
+                nc.tensor.transpose(tts[b][:, j, :], toks[b][:, j * P : (j + 1) * P], ident[:])
 
         def tcl(b):
-            nc.scalar.copy(out=tcol[b][:], in_=tts[b][:, :, P - 1])
+            nc.scalar.activation(out=tcol(b)[:], in_=tts[b][:, :, P - 1], func=ACT.Copy)
 
         def spt(b):
-            t = psum.tile([P, 4, P], F32, name="sp", tag=f"acc{b}0")
-            for j in range(4):
-                nc.tensor.transpose(t[:, j, :], tcol[b][:, j : j + 1].to_broadcast([P, P]), ident_f[:])
-            tts[b] = t
+            tts[b] = psum.tile([P, PACK, P], F32, name="spread", tag=f"turn{2 + b}")
+            for j in range(PACK):
+                nc.tensor.transpose(tts[b][:, j, :], tcol(b)[:, j : j + 1].to_broadcast([P, P]), ident[:])
 
         def spc(b):
-            if "trow" not in late:
-                late["trow"] = keep.tile([P, B, N], F32, name="trow", tag="trow", align_bytes=64)
             nc.scalar.copy(
-                out=late["trow"][:, b].rearrange("q (s j) -> q s j", j=4), in_=tts[b][:].rearrange("q j s -> q s j")
+                out=trow(b)[:].rearrange("q (s j) -> q s j", j=PACK), in_=tts[b][:].rearrange("q j s -> q s j")
             )
 
         def sca(b, h):
-            cols = slice(h * 256, (h + 1) * 256)
-            nc.vector.tensor_tensor(
-                out=a[b][:, cols],
-                in0=scores[b, h][:],
-                in1=late["trow"][:, b, cols],
-                op=ALU.mult,
-            )
+            cols = slice(h * HALF, (h + 1) * HALF)
+            nc.vector.tensor_tensor(out=a[b][:, cols], in0=scores[b, h][:], in1=trow(b)[:, cols], op=ALU.mult)
 
         def mx(b):
-            neg_m[b] = keep.tile([P, 1], F32, name=f"nm{b}")
-            nc.vector.tensor_reduce(
-                out=neg_m[b][:],
-                in_=a[b][:],
-                axis=mybir.AxisListType.X,
-                op=ALU.max,
-                negate=True,
-            )
+            nc.vector.tensor_reduce(out=neg_m[b][:], in_=a[b][:], axis=mybir.AxisListType.X, op=ALU.max, negate=True)
 
         def ex(b, h):
             nc.scalar.activation(
                 out=p[b][:, 2 * h : 2 * h + 2, :].rearrange("q j s -> q s j"),
-                in_=a[b][:].rearrange("q (s j) -> q s j", j=4)[:, :, 2 * h : 2 * h + 2],
+                in_=a[b][:].rearrange("q (s j) -> q s j", j=PACK)[:, :, 2 * h : 2 * h + 2],
                 func=ACT.Exp,
                 bias=neg_m[b][:],
                 scale=1.0,
@@ -235,24 +225,20 @@ def tile_attend_mla_kernel(tc, qT, cT, ts, ch, offs, out):
 
         def pt(b, h):
             if h == 0:
-                pts[b] = psum.tile([P, 4, P], F32, name="pt", tag=("bank00", "bank11")[b])
+                pts[b] = psum.tile([P, PACK, P], F32, name="pt", tag=f"turn{b}")
             for j in range(2 * h, 2 * h + 2):
-                nc.tensor.transpose(pts[b][:, j, :], p[b][:, j, :], ident_f[:])
+                nc.tensor.transpose(pts[b][:, j, :], p[b][:, j, :], ident[:])
 
         def w(b):
-            wts[b] = keep.tile([P, NQ, 4], BF16, name=f"w{b}", tag="w", align_bytes=64)
             nc.vector.tensor_tensor(
                 out=wts[b][:],
                 in0=pts[b][:].rearrange("s j q -> s q j"),
-                in1=tcol[b][:].unsqueeze(1).to_broadcast([P, NQ, 4]),
+                in1=tcol(b)[:].unsqueeze(1).to_broadcast([P, NQ, PACK]),
                 op=ALU.mult,
             )
 
         def qw(b):
-            wq = keep.tile([P, NQ], U32, name=f"wq{b}", align_bytes=64)
-            ws = keep.tile([P, NQ], U8, name=f"ws{b}", align_bytes=64)
-            nc.vector.quantize_mx(out=wq[:].bitcast(FP8X4), scales=ws[:], in_=wts[b][:].rearrange("s q j -> s (q j)"))
-            wqs[b] = (wq, ws)
+            nc.vector.quantize_mx(out=wq[b][:].bitcast(FP8X4), scales=ws[b][:], in_=wts[b][:].rearrange("s q j -> s (q j)"))
 
         def rec():
             nc.vector.tensor_reduce(out=total[:], in_=parts[:], axis=mybir.AxisListType.X, op=ALU.add)
@@ -260,26 +246,25 @@ def tile_attend_mla_kernel(tc, qT, cT, ts, ch, offs, out):
 
         def mix(b, h):
             cols = slice(h * 2 * P, (h + 1) * 2 * P)
-            wq, ws = wqs[b]
             ys[b, h] = psum.tile([P, 2 * P], F32, name="y", tag=f"acc{b}{h}")
             nc.tensor.matmul_mx(
                 out=ys[b, h][:],
-                lhsT=wq[:].bitcast(FP8X4),
-                lhsT_scale=ws[:],
-                rhs=vq[b][:, cols].bitcast(FP8X4),
-                rhs_scale=vs[:, b, cols],
+                lhsT=wq[b][:].bitcast(FP8X4),
+                lhsT_scale=ws[b][:],
+                rhs=vq(b)[:, cols].bitcast(FP8X4),
+                rhs_scale=vs[b][:, cols],
                 start=True,
                 stop=True,
             )
 
-        def fin(b, h, first, count):
-            cols = slice(h * 2 * P + 4 * first, h * 2 * P + 4 * (first + count))
-            o = keep.tile([P, 4 * count], F32, name=f"o{b}{h}{first}")
+        def fin(b, first, count):
+            cols = slice(PACK * first, PACK * (first + count))
+            o = keep.tile([P, PACK * count], F32, name=f"o{b}{first}")
             nc.vector.scalar_tensor_tensor(
-                out=o[:].rearrange("q (p f) -> q p f", f=4),
-                in0=ys[b, h][:].rearrange("q (f p) -> q p f", f=4)[:, first : first + count, :],
+                out=o[:].rearrange("q (p t) -> q p t", t=PACK),
+                in0=ys[b, first // 64][:].rearrange("q (t p) -> q p t", t=PACK)[:, first % 64 : first % 64 + count, :],
                 scalar=inv[:, b : b + 1],
-                in1=ch_sb[:, cols].rearrange("q (p f) -> q p f", f=4),
+                in1=ch_sb[:, cols].rearrange("q (p t) -> q p t", t=PACK),
                 op0=ALU.mult,
                 op1=ALU.mult,
             )
@@ -290,79 +275,81 @@ def tile_attend_mla_kernel(tc, qT, cT, ts, ch, offs, out):
         tt(0)
         tcl(0)
         spt(0)
-        spc(0)
         tt(1)
-        cv(0)
-        cs(0)
+        gather(0, 0, 0, N, False)
+        gather(1, 0, 0, N, True)
         tcl(1)
         spt(1)
-        spc(1)
-        g(0, 0)
-        g(1, 0)
-        cs(1)
+        spc(0)
         tv(0, 0)
-        vc(0, 0, 0)
-        vc(0, 0, 1)
         tv(1, 0)
-        cv(2)
-        cv(3)
-        gh(0, 0)
-        gh(0, 1)
-        gh(1, 0)
-        gh(1, 1)
-        qc(0)
-        qc(1)
-        ilv(0, 0)
-        ilv(0, 1)
-        ilv(1, 0)
-        ilv(1, 1)
-        qQ(0)
-        qK(0, 0)
-        mm(0, 0)
-        qK(0, 1)
-        mm(0, 1)
-        qQ(1)
-        qK(1, 0)
-        mm(1, 0)
-        qK(1, 1)
-        mm(1, 1)
+        gather(0, 1, 0, N, False)
+        gather(1, 1, 0, N, True)
+        spc(1)
+        weave(0, 0, 0, N)
+        weave(1, 0, 0, N)
         tv(0, 1)
         tv(1, 1)
+        gather(0, 2, 0, N, False)
+        gather(1, 2, 0, N, True)
+        tv(0, 2)
+        tv(1, 2)
+        gather(0, 3, 0, P, False)
+        gather(0, 3, P, P, False)
+        gather(0, 3, HALF, HALF, True)
+        gather(1, 3, 0, HALF, True)
+        qc(0)
+        gather(1, 3, HALF, HALF, True)
+        qc(1)
+        tv(0, 3)
+        tv(1, 3)
+        weave(0, 1, 0, P)
+        weave(0, 1, P, P)
+        weave(0, 1, HALF, HALF)
+        weave(1, 1, 0, HALF)
+        qK(0, 0, N)
+        qQ(0)
+        mm(0, 0)
+        mm(0, 1)
+        weave(1, 1, HALF, HALF)
+        qK(1, 0, HALF)
+        qQ(1)
+        mm(1, 0)
+        qK(1, HALF, HALF)
+        mm(1, 1)
+        vc(0)
+        vc(1)
+        vc(2)
+        vc(3)
         sca(0, 0)
         sca(0, 1)
+        sca(1, 0)
+        sca(1, 1)
         mx(0)
+        mx(1)
         ex(0, 0)
         pt(0, 0)
         ex(0, 1)
         pt(0, 1)
-        sca(1, 0)
-        sca(1, 1)
-        mx(1)
         ex(1, 0)
         pt(1, 0)
         ex(1, 1)
         pt(1, 1)
-        vc(0, 1, 0)
-        vc(0, 1, 1)
-        vc(1, 0, 0)
-        vc(1, 0, 1)
-        vc(1, 1, 0)
-        vc(1, 1, 1)
-        rec()
         w(0)
-        qw(0)
         qv(0, 0)
+        qw(0)
         qv(0, 1)
         mix(0, 0)
         mix(0, 1)
+        rec()
         w(1)
-        qw(1)
         qv(1, 0)
+        qw(1)
         qv(1, 1)
         mix(1, 0)
         mix(1, 1)
-        fin(0, 0, 0, 64)
-        fin(0, 1, 0, 64)
-        fin(1, 0, 0, 64)
-        fin(1, 1, 0, 32)
-        fin(1, 1, 32, 32)
+        fin(0, 0, 64)
+        fin(0, 64, 64)
+        fin(1, 0, 64)
+        fin(1, 64, 32)
+        fin(1, 96, 32)

@@ -18,7 +18,7 @@ FP8X4 = mybir.dt.float8_e4m3fn_x4
 ACT = mybir.ActivationFunctionType
 ALU = mybir.AluOpType
 
-HEAD = 512
+HEAD = 1024
 KB = 1024
 PLANE_AT = [8 * KB * t for t in range(PACK)]
 QRAW_AT = [32 * KB + 2 * KB * b for b in range(B)]
@@ -145,11 +145,11 @@ def tile_attend_mla_kernel(tc, qT, cT, ts, ch, offs, out):
                 in_=turned[t][:].rearrange("s b u (h p) -> s b h p u", h=2),
             )
 
-        def qv(b, h):
-            cols = slice(h * 2 * P, (h + 1) * 2 * P)
-            at = (2 * b + h) * 2 * P * PACK
+        def qv(b, quarter):
+            cols = slice(quarter * P, (quarter + 1) * P)
+            at = (PACK * b + quarter) * P * PACK
             nc.vector.quantize_mx(
-                out=vq(b)[:, cols].bitcast(FP8X4), scales=vs[b][:, cols], in_=vals()[:, at : at + 2 * P * PACK]
+                out=vq(b)[:, cols].bitcast(FP8X4), scales=vs[b][:, cols], in_=vals()[:, at : at + P * PACK]
             )
 
         def qc(b):
@@ -240,8 +240,12 @@ def tile_attend_mla_kernel(tc, qT, cT, ts, ch, offs, out):
         def qw(b):
             nc.vector.quantize_mx(out=wq[b][:].bitcast(FP8X4), scales=ws[b][:], in_=wts[b][:].rearrange("s q j -> s (q j)"))
 
+        def row_sum(b):
+            nc.scalar.activation(
+                out=total[:, b : b + 1], in_=parts[:, b, 0:1], func=ACT.Identity, bias=parts[:, b, 1:2], scale=1.0
+            )
+
         def rec():
-            nc.vector.tensor_reduce(out=total[:], in_=parts[:], axis=mybir.AxisListType.X, op=ALU.add)
             nc.vector.reciprocal(out=inv[:], in_=total[:])
 
         def mix(b, h):
@@ -324,8 +328,8 @@ def tile_attend_mla_kernel(tc, qT, cT, ts, ch, offs, out):
         sca(0, 0)
         sca(0, 1)
         sca(1, 0)
-        sca(1, 1)
         mx(0)
+        sca(1, 1)
         mx(1)
         ex(0, 0)
         pt(0, 0)
@@ -335,17 +339,23 @@ def tile_attend_mla_kernel(tc, qT, cT, ts, ch, offs, out):
         pt(1, 0)
         ex(1, 1)
         pt(1, 1)
+        row_sum(0)
+        row_sum(1)
         w(0)
-        qv(0, 0)
         qw(0)
+        w(1)
+        qw(1)
+        qv(0, 0)
         qv(0, 1)
+        qv(0, 2)
+        qv(0, 3)
         mix(0, 0)
         mix(0, 1)
-        rec()
-        w(1)
         qv(1, 0)
-        qw(1)
         qv(1, 1)
+        qv(1, 2)
+        qv(1, 3)
+        rec()
         mix(1, 0)
         mix(1, 1)
         fin(0, 0, 64)

@@ -18,21 +18,49 @@ FP8X4 = mybir.dt.float8_e4m3fn_x4
 ACT = mybir.ActivationFunctionType
 ALU = mybir.AluOpType
 
-HEAD = 1024
+HEAD = 512
 KB = 1024
 PLANE_AT = [8 * KB * t for t in range(PACK)]
-QRAW_AT = [32 * KB + 2 * KB * b for b in range(B)]
+QRAW_AT = [32 * KB, 36 * KB]
 TOKS_AT = [44 * KB + 2 * KB * b for b in range(B)]
 SPARE_AT = 48 * KB
+GROUPS = [[[0], [1], [2], [3]], [[0, 1], [2, 3]]]
+CUTS = [2, 4]
 LIES_ON = {
     "picked10": TOKS_AT[0],
-    "tcol1": PLANE_AT[0],
+    "vals00": SPARE_AT,
+    "picked1": SPARE_AT,
     "q_sb1": PLANE_AT[3] + KB,
-    "vals": QRAW_AT[1] + KB,
+    "vals02": QRAW_AT[1] + KB - 64,
+    "vals03": QRAW_AT[1] - 64,
+    "tcol1": QRAW_AT[1] + 2 * KB - 64,
     "kq1": QRAW_AT[0],
-    "trow1": SPARE_AT + KB,
-    "vq0": SPARE_AT,
-    "vq1": SPARE_AT + 2 * KB,
+    "vals11": QRAW_AT[0],
+}
+BANK = {
+    "dealt0": 0,
+    "spread0": 1,
+    "natural": 2,
+    "turned0": 0,
+    "turned1": 2,
+    "turned2": 1,
+    "dealt1": 0,
+    "turned3": 3,
+    "scores00": 4,
+    "scores01": 5,
+    "slots0": 6,
+    "slots1": 7,
+    "slots2": 2,
+    "slots3": 0,
+    "a1": 6,
+    "pt0": 7,
+    "pt1": 2,
+    "y00": 4,
+    "y01": 5,
+    "y10": 0,
+    "y11": 1,
+    "y12": 3,
+    "y13": 6,
 }
 
 
@@ -65,21 +93,11 @@ def tile_attend_mla_kernel(tc, qT, cT, ts, ch, offs, out):
         ch_sb = keep.tile([P, DV], F32, name="ch_sb")
         nc.sync.dma_start(out=ch_sb[:], in_=ch)
 
-        ks = [keep.tile([P, N], U8, name=f"ks{b}", align_bytes=64) for b in range(B)]
-        vs = [keep.tile([P, DV], U8, name=f"vs{b}", align_bytes=64) for b in range(B)]
-        qq = [keep.tile([P, NQ], U32, name=f"qq{b}", align_bytes=64) for b in range(B)]
-        qs = [keep.tile([P, NQ], U8, name=f"qs{b}", align_bytes=64) for b in range(B)]
         toks = [over.tile([P, N], F32, name=f"toks{b}", align_bytes=64, offset=TOKS_AT[b]) for b in range(B)]
-        a = [keep.tile([P, N], F32, name=f"a{b}") for b in range(B)]
-        p = [keep.tile([P, PACK, P], F32, name=f"p{b}") for b in range(B)]
-        neg_m = [keep.tile([P, 1], F32, name=f"neg_m{b}") for b in range(B)]
-        parts = keep.tile([P, B, 2], F32, name="parts")
+        parts = keep.tile([P, B, PACK], F32, name="parts")
         total = keep.tile([P, B], F32, name="total")
         inv = keep.tile([P, B], F32, name="inv")
-        wts = [keep.tile([P, NQ, PACK], BF16, name=f"w{b}", align_bytes=64) for b in range(B)]
-        wq = [keep.tile([P, NQ], U32, name=f"wq{b}", align_bytes=64) for b in range(B)]
-        ws = [keep.tile([P, NQ], U8, name=f"ws{b}", align_bytes=64) for b in range(B)]
-        turned, scores, tts, pts, ys, made = ({} for i in range(6))
+        made = {}
 
         def late(name, width, dt):
             if name not in made:
@@ -89,29 +107,39 @@ def tile_attend_mla_kernel(tc, qT, cT, ts, ch, offs, out):
                     made[name] = keep.tile([P, width], dt, name=name, align_bytes=64)
             return made[name]
 
-        def tcol(b):
-            return late(f"tcol{b}", PACK, F32)
-
-        def trow(b):
-            return late(f"trow{b}", N, F32)
+        def bank(name, width=N):
+            if name not in made:
+                made[name] = psum.tile([P, width], F32, name=name, tag=f"bank{BANK[name]}")
+            return made[name]
 
         def picked(b, u):
-            return late(f"picked{b}{u}", 2 * N, BF16)
+            if u == 0:
+                return late(f"picked{b}0", 2 * N, BF16)
+            return late("picked1", B * 2 * N, BF16)[:, b * 2 * N : (b + 1) * 2 * N]
 
         def keys(b):
             return late(f"keys{b}", N * PACK, BF16)
 
-        def vals():
-            return late("vals", B * DV * PACK, BF16)
+        def vals(b, g):
+            return late(f"vals{b}{g}", DV * len(GROUPS[b][g]), BF16)
 
-        def vq(b):
-            return late(f"vq{b}", DV, U32)
+        def codes(kind, b, width):
+            return late(f"{kind}q{b}", width, U32), late(f"{kind}s{b}", width, U8)
 
-        def kq(b):
-            return late(f"kq{b}", N, U32)
+        def quantise(kind, b, width, cols, src):
+            words, scales = codes(kind, b, width)
+            nc.vector.quantize_mx(out=words[:, cols].bitcast(FP8X4), scales=scales[:, cols], in_=src)
 
-        def q_sb(b):
-            return late(f"q_sb{b}", NQ * PACK, BF16)
+        def product(dst, left, left_cols, right, right_cols):
+            nc.tensor.matmul_mx(
+                out=dst,
+                lhsT=left[0][:, left_cols].bitcast(FP8X4),
+                lhsT_scale=left[1][:, left_cols],
+                rhs=right[0][:, right_cols].bitcast(FP8X4),
+                rhs_scale=right[1][:, right_cols],
+                start=True,
+                stop=True,
+            )
 
         def entries(b, first, count):
             col = (b * N + first) // 16
@@ -126,61 +154,47 @@ def tile_attend_mla_kernel(tc, qT, cT, ts, ch, offs, out):
             else:
                 nc.vector.tensor_copy(out=dst, in_=src)
 
-        def weave(b, u, first, count):
-            nc.vector.tensor_copy(
+        def weave(b, u, first, count, on_scalar=False):
+            (nc.scalar.copy if on_scalar else nc.vector.tensor_copy)(
                 out=keys(b)[:].rearrange("p (n t) -> p n t", t=PACK)[:, first : first + count, 2 * u : 2 * u + 2],
-                in_=picked(b, u)[:].rearrange("p (e n) -> p n e", e=2)[:, first : first + count, :],
+                in_=picked(b, u)[:, :].rearrange("p (e n) -> p n e", e=2)[:, first : first + count, :],
             )
 
         def tv(b, t):
-            if b == 0:
-                turned[t] = psum.tile([P, B, 2, P], F32, name="turned", tag=f"turn{t}")
+            turned = bank(f"turned{t}")[:].rearrange("s (b u p) -> s b u p", b=B, u=2)
             words = picked(b, t // 2)[:, (t % 2) * N : (t % 2 + 1) * N].bitcast(F32).rearrange("p (s u) -> p u s", u=2)
             for u in range(2):
-                nc.tensor.transpose(turned[t][:, b, u, :], words[:, u, :], ident[:])
+                nc.tensor.transpose(turned[:, b, u, :], words[:, u, :], ident[:])
 
-        def vc(t):
+        def vc(b, g, e):
+            count = len(GROUPS[b][g])
             nc.scalar.copy(
-                out=vals()[:].bitcast(F32).rearrange("s (b h t p u) -> s t b h p u", b=B, h=2, t=PACK, u=2)[:, t],
-                in_=turned[t][:].rearrange("s b u (h p) -> s b h p u", h=2),
+                out=vals(b, g)[:].bitcast(F32).rearrange("s (c e p u) -> s e c p u", c=CUTS[b], e=count, u=2)[:, e],
+                in_=bank(f"turned{GROUPS[b][g][e]}")[:].rearrange("s (b u c p) -> s b c p u", b=B, u=2, c=CUTS[b])[:, b],
             )
 
-        def qv(b, quarter):
-            cols = slice(quarter * P, (quarter + 1) * P)
-            at = (PACK * b + quarter) * P * PACK
-            nc.vector.quantize_mx(
-                out=vq(b)[:, cols].bitcast(FP8X4), scales=vs[b][:, cols], in_=vals()[:, at : at + P * PACK]
-            )
+        def qv(b, c, g):
+            width = len(GROUPS[b][g]) * P // CUTS[b]
+            first = c * DV // CUTS[b] + GROUPS[b][g][0] * P // CUTS[b]
+            quantise("v", b, DV, slice(first, first + width), vals(b, g)[:, c * width * PACK : (c + 1) * width * PACK])
 
         def qc(b):
             nc.scalar.copy(
-                out=q_sb(b)[:].rearrange("p (c i t) -> p c t i", i=4, t=PACK),
+                out=late(f"q_sb{b}", NQ * PACK, BF16)[:].rearrange("p (c i t) -> p c t i", i=4, t=PACK),
                 in_=q_raw[b][:].rearrange("p t (c i) -> p c t i", i=4),
             )
 
         def qQ(b):
-            nc.vector.quantize_mx(out=qq[b][:].bitcast(FP8X4), scales=qs[b][:], in_=q_sb(b)[:])
+            quantise("q", b, NQ, slice(0, NQ), late(f"q_sb{b}", NQ * PACK, BF16)[:])
 
         def qK(b, first, count):
-            cols = slice(first, first + count)
-            nc.vector.quantize_mx(
-                out=kq(b)[:, cols].bitcast(FP8X4),
-                scales=ks[b][:, cols],
-                in_=keys(b)[:, PACK * first : PACK * (first + count)],
-            )
+            quantise("k", b, N, slice(first, first + count), keys(b)[:, PACK * first : PACK * (first + count)])
 
         def mm(b, h):
-            cols = slice(h * HALF, (h + 1) * HALF)
-            scores[b, h] = psum.tile([P, HALF], F32, name="scores", tag=f"acc{b}{h}")
-            nc.tensor.matmul_mx(
-                out=scores[b, h][:],
-                lhsT=qq[b][:].bitcast(FP8X4),
-                lhsT_scale=qs[b][:],
-                rhs=kq(b)[:, cols].bitcast(FP8X4),
-                rhs_scale=ks[b][:, cols],
-                start=True,
-                stop=True,
-            )
+            product(bank(f"scores{b}{h}", HALF)[:], codes("q", b, NQ), slice(0, NQ), codes("k", b, N), slice(h * HALF, (h + 1) * HALF))
+
+        def mm1(j):
+            product(bank(f"slots{j}", NQ)[:], codes("k", 1, N), slice(j * P, (j + 1) * P), codes("q", 1, NQ), slice(0, NQ))
 
         def tok(b):
             nc.vector.tensor_copy(
@@ -188,112 +202,136 @@ def tile_attend_mla_kernel(tc, qT, cT, ts, ch, offs, out):
                 in_=ts_sb[:].bitcast(U32).indirect(entries(b, 0, N)),
             )
 
-        def tt(b):
-            tts[b] = psum.tile([P, PACK, P], F32, name="tt", tag=f"turn{b}")
-            for j in range(PACK):
-                nc.tensor.transpose(tts[b][:, j, :], toks[b][:, j * P : (j + 1) * P], ident[:])
+        def tok1():
+            nc.vector.tensor_copy(out=toks[1][:], in_=ts_sb[:].indirect(entries(1, 0, N)))
 
-        def tcl(b):
-            nc.scalar.activation(out=tcol(b)[:], in_=tts[b][:, :, P - 1], func=ACT.Copy)
+        def tt(name, src):
+            for j in range(PACK):
+                nc.tensor.transpose(bank(name)[:, j * P : (j + 1) * P], src[:, j, :], ident[:])
+
+        def tcl(name, col):
+            nc.scalar.activation(
+                out=late(col, PACK, F32)[:], in_=bank(name)[:].rearrange("s (j q) -> s j q", j=PACK)[:, :, P - 1], func=ACT.Copy
+            )
 
         def spt(b):
-            tts[b] = psum.tile([P, PACK, P], F32, name="spread", tag=f"turn{2 + b}")
             for j in range(PACK):
-                nc.tensor.transpose(tts[b][:, j, :], tcol(b)[:, j : j + 1].to_broadcast([P, P]), ident[:])
+                nc.tensor.transpose(
+                    bank(f"spread{b}")[:, j * P : (j + 1) * P], late(f"tcol{b}", PACK, F32)[:, j : j + 1].to_broadcast([P, P]), ident[:]
+                )
 
         def spc(b):
-            nc.scalar.copy(
-                out=trow(b)[:].rearrange("q (s j) -> q s j", j=PACK), in_=tts[b][:].rearrange("q j s -> q s j")
-            )
+            nc.scalar.copy(out=late(f"trow{b}", N, F32)[:], in_=bank(f"spread{b}")[:])
 
         def sca(b, h):
-            cols = slice(h * HALF, (h + 1) * HALF)
-            nc.vector.tensor_tensor(out=a[b][:, cols], in0=scores[b, h][:], in1=trow(b)[:, cols], op=ALU.mult)
-
-        def mx(b):
-            nc.vector.tensor_reduce(out=neg_m[b][:], in_=a[b][:], axis=mybir.AxisListType.X, op=ALU.max, negate=True)
-
-        def ex(b, h):
-            nc.scalar.activation(
-                out=p[b][:, 2 * h : 2 * h + 2, :].rearrange("q j s -> q s j"),
-                in_=a[b][:].rearrange("q (s j) -> q s j", j=PACK)[:, :, 2 * h : 2 * h + 2],
-                func=ACT.Exp,
-                bias=neg_m[b][:],
-                scale=1.0,
-                accum_out=parts[:, b, h : h + 1],
+            part = slice(h * P // 2, (h + 1) * P // 2)
+            nc.vector.tensor_tensor(
+                out=late(f"a{b}s", N, F32)[:].rearrange("q (j s) -> q j s", j=PACK)[:, :, part],
+                in0=bank(f"scores{b}{h}")[:].rearrange("q (s j) -> q j s", j=PACK),
+                in1=late(f"trow{b}", N, F32)[:].rearrange("q (j s) -> q j s", j=PACK)[:, :, part],
+                op=ALU.mult,
             )
 
-        def pt(b, h):
-            if h == 0:
-                pts[b] = psum.tile([P, PACK, P], F32, name="pt", tag=f"turn{b}")
-            for j in range(2 * h, 2 * h + 2):
-                nc.tensor.transpose(pts[b][:, j, :], p[b][:, j, :], ident[:])
+        def sca1(j):
+            nc.scalar.activation(
+                out=late(f"scaled{j}", NQ, F32)[:], in_=bank(f"slots{j}")[:], func=ACT.Copy, scale=late("tnat", PACK, F32)[:, j : j + 1]
+            )
+
+        def ta(j):
+            nc.tensor.transpose(bank("a1")[:, j * P : (j + 1) * P], late(f"scaled{j}", NQ, F32)[:], ident[:])
+
+        def a(b):
+            if b:
+                return bank("a1")[:].rearrange("q (s j) -> q j s", j=PACK)
+            return late(f"a{b}s", N, F32)[:].rearrange("q (j s) -> q j s", j=PACK)
+
+        def mx(b):
+            nc.vector.tensor_reduce(
+                out=late(f"neg_m{b}", 1, F32)[:], in_=bank("a1")[:] if b else late("a0s", N, F32)[:], axis=mybir.AxisListType.X, op=ALU.max, negate=True
+            )
+
+        def ex(b, part, first, count):
+            nc.scalar.activation(
+                out=late(f"p{b}", N, F32)[:].rearrange("q (j s) -> q j s", j=PACK)[:, first : first + count, :],
+                in_=a(b)[:, first : first + count, :],
+                func=ACT.Exp,
+                bias=late(f"neg_m{b}", 1, F32)[:],
+                scale=1.0,
+                accum_out=parts[:, b, part : part + 1],
+            )
+            for j in range(first, first + count):
+                cols = slice(j * P, (j + 1) * P)
+                nc.tensor.transpose(bank(f"pt{b}")[:, cols], late(f"p{b}", N, F32)[:, cols], ident[:])
 
         def w(b):
             nc.vector.tensor_tensor(
-                out=wts[b][:],
-                in0=pts[b][:].rearrange("s j q -> s q j"),
-                in1=tcol(b)[:].unsqueeze(1).to_broadcast([P, NQ, PACK]),
+                out=late(f"w{b}", NQ * PACK, BF16)[:].rearrange("s (q j) -> s q j", j=PACK),
+                in0=bank(f"pt{b}")[:].rearrange("s (j q) -> s q j", j=PACK),
+                in1=late(f"tcol{b}", PACK, F32)[:].unsqueeze(1).to_broadcast([P, NQ, PACK]),
                 op=ALU.mult,
             )
 
         def qw(b):
-            nc.vector.quantize_mx(out=wq[b][:].bitcast(FP8X4), scales=ws[b][:], in_=wts[b][:].rearrange("s q j -> s (q j)"))
+            quantise("w", b, NQ, slice(0, NQ), late(f"w{b}", NQ * PACK, BF16)[:])
 
         def row_sum(b):
             nc.scalar.activation(
                 out=total[:, b : b + 1], in_=parts[:, b, 0:1], func=ACT.Identity, bias=parts[:, b, 1:2], scale=1.0
             )
 
+        def row_sums():
+            nc.vector.tensor_reduce(out=total[:], in_=parts[:], axis=mybir.AxisListType.X, op=ALU.add)
+
         def rec():
             nc.vector.reciprocal(out=inv[:], in_=total[:])
 
-        def mix(b, h):
-            cols = slice(h * 2 * P, (h + 1) * 2 * P)
-            ys[b, h] = psum.tile([P, 2 * P], F32, name="y", tag=f"acc{b}{h}")
-            nc.tensor.matmul_mx(
-                out=ys[b, h][:],
-                lhsT=wq[b][:].bitcast(FP8X4),
-                lhsT_scale=ws[b][:],
-                rhs=vq(b)[:, cols].bitcast(FP8X4),
-                rhs_scale=vs[b][:, cols],
-                start=True,
-                stop=True,
-            )
+        def mix(b, c):
+            width = DV // CUTS[b]
+            product(bank(f"y{b}{c}", width)[:], codes("w", b, NQ), slice(0, NQ), codes("v", b, DV), slice(c * width, (c + 1) * width))
 
-        def fin(b, first, count):
-            cols = slice(PACK * first, PACK * (first + count))
-            o = keep.tile([P, PACK * count], F32, name=f"o{b}{first}")
+        def fin(b, c):
+            width = DV // CUTS[b]
+            cols = slice(c * width, (c + 1) * width)
             nc.vector.scalar_tensor_tensor(
-                out=o[:].rearrange("q (p t) -> q p t", t=PACK),
-                in0=ys[b, first // 64][:].rearrange("q (t p) -> q p t", t=PACK)[:, first % 64 : first % 64 + count, :],
+                out=late(f"o{b}", DV, F32)[:, cols].rearrange("q (p t) -> q p t", t=PACK),
+                in0=bank(f"y{b}{c}")[:].rearrange("q (t p) -> q p t", t=PACK),
                 scalar=inv[:, b : b + 1],
                 in1=ch_sb[:, cols].rearrange("q (p t) -> q p t", t=PACK),
                 op0=ALU.mult,
                 op1=ALU.mult,
             )
-            nc.sync.dma_start(out=out[b][:, cols], in_=o[:])
+
+        def store(b, first, count):
+            nc.sync.dma_start(out=out[b][:, first : first + count], in_=late(f"o{b}", DV, F32)[:, first : first + count])
 
         tok(0)
-        tok(1)
-        tt(0)
-        tcl(0)
+        tok1()
+        tt("dealt0", toks[0][:].rearrange("q (j s) -> q j s", j=PACK))
+        tcl("dealt0", "tcol0")
         spt(0)
-        tt(1)
+        tt("natural", toks[1][:].rearrange("q (j s) -> q j s", j=PACK))
         gather(0, 0, 0, N, False)
         gather(1, 0, 0, N, True)
-        tcl(1)
-        spt(1)
-        spc(0)
+        tcl("natural", "tnat")
         tv(0, 0)
         tv(1, 0)
         gather(0, 1, 0, N, False)
         gather(1, 1, 0, N, True)
-        spc(1)
+        vc(0, 0, 0)
+        vc(1, 0, 0)
+        spc(0)
         weave(0, 0, 0, N)
         weave(1, 0, 0, N)
         tv(0, 1)
         tv(1, 1)
+        vc(0, 1, 0)
+        vc(1, 0, 1)
+        tt("dealt1", toks[1][:].rearrange("q (s j) -> q j s", j=PACK))
+        qv(0, 0, 0)
+        qv(0, 1, 0)
+        qv(0, 0, 1)
+        qv(0, 1, 1)
+        for c in range(PACK): qv(1, c, 0)
         gather(0, 2, 0, N, False)
         gather(1, 2, 0, N, True)
         tv(0, 2)
@@ -302,9 +340,10 @@ def tile_attend_mla_kernel(tc, qT, cT, ts, ch, offs, out):
         gather(0, 3, P, P, False)
         gather(0, 3, HALF, HALF, True)
         gather(1, 3, 0, HALF, True)
-        qc(0)
         gather(1, 3, HALF, HALF, True)
+        qc(0)
         qc(1)
+        weave(1, 1, 3 * P, P, True)
         tv(0, 3)
         tv(1, 3)
         weave(0, 1, 0, P)
@@ -315,51 +354,57 @@ def tile_attend_mla_kernel(tc, qT, cT, ts, ch, offs, out):
         qQ(0)
         mm(0, 0)
         mm(0, 1)
-        weave(1, 1, HALF, HALF)
-        qK(1, 0, HALF)
+        weave(1, 1, HALF, P)
+        qK(1, 0, P)
         qQ(1)
-        mm(1, 0)
-        qK(1, HALF, HALF)
-        mm(1, 1)
-        vc(0)
-        vc(1)
-        vc(2)
-        vc(3)
+        mm1(0)
+        qK(1, P, P)
+        mm1(1)
+        tcl("dealt1", "tcol1")
+        vc(0, 2, 0)
+        vc(0, 3, 0)
+        qK(1, 2 * P, P)
+        mm1(2)
+        qK(1, 3 * P, P)
+        mm1(3)
         sca(0, 0)
         sca(0, 1)
-        sca(1, 0)
         mx(0)
-        sca(1, 1)
+        sca1(0)
+        ta(0)
+        sca1(1)
+        ta(1)
+        sca1(2)
+        ta(2)
+        sca1(3)
+        ta(3)
+        vc(1, 1, 0)
+        vc(1, 1, 1)
         mx(1)
-        ex(0, 0)
-        pt(0, 0)
-        ex(0, 1)
-        pt(0, 1)
-        ex(1, 0)
-        pt(1, 0)
-        ex(1, 1)
-        pt(1, 1)
-        row_sum(0)
-        row_sum(1)
+        for j in range(PACK): ex(0, j, j, 1)
+        for j in range(PACK): ex(1, j, j, 1)
         w(0)
         qw(0)
         w(1)
         qw(1)
-        qv(0, 0)
-        qv(0, 1)
-        qv(0, 2)
-        qv(0, 3)
+        qv(0, 0, 2)
+        qv(0, 1, 2)
+        qv(0, 0, 3)
+        qv(0, 1, 3)
         mix(0, 0)
         mix(0, 1)
-        qv(1, 0)
-        qv(1, 1)
-        qv(1, 2)
-        qv(1, 3)
+        for c in range(PACK): qv(1, c, 1)
+        row_sums()
         rec()
-        mix(1, 0)
-        mix(1, 1)
-        fin(0, 0, 64)
-        fin(0, 64, 64)
-        fin(1, 0, 64)
-        fin(1, 64, 32)
-        fin(1, 96, 32)
+        for c in range(PACK): mix(1, c)
+        fin(0, 0)
+        store(0, 0, HALF)
+        fin(0, 1)
+        store(0, HALF, HALF)
+        fin(1, 0)
+        fin(1, 1)
+        store(1, 0, HALF)
+        fin(1, 2)
+        store(1, HALF, P)
+        fin(1, 3)
+        store(1, 3 * P, P)

@@ -20,20 +20,26 @@ ALU = mybir.AluOpType
 
 HEAD = 512
 KB = 1024
+EXP_RUNS = [(0, 2), (2, 1), (3, 1)]
 PLANE_AT = [8 * KB * t for t in range(PACK)]
 QRAW_AT = [32 * KB, 36 * KB]
 TOKS_AT = [44 * KB + 2 * KB * b for b in range(B)]
 SPARE_AT = 48 * KB
-GROUPS = [[[0], [1], [2], [3]], [[0, 1], [2, 3]]]
-CUTS = [2, 4]
+SCALED_AT = 54 * KB
+ROW_AT = 56 * KB
+COLUMN_AT = 60 * KB
 LIES_ON = {
     "picked10": TOKS_AT[0],
     "vals00": SPARE_AT,
     "picked1": SPARE_AT,
     "q_sb1": PLANE_AT[3] + KB,
-    "vals02": QRAW_AT[1] + KB - 64,
-    "vals03": QRAW_AT[1] - 64,
-    "tcol1": QRAW_AT[1] + 2 * KB - 64,
+    "vals01": QRAW_AT[1],
+    "scaled3": SCALED_AT,
+    "v1s1": SCALED_AT,
+    "tcol0": COLUMN_AT,
+    "w1": COLUMN_AT,
+    "keys1": ROW_AT,
+    "v1s0": ROW_AT,
     "kq1": QRAW_AT[0],
     "vals11": QRAW_AT[0],
 }
@@ -43,11 +49,10 @@ BANK = {
     "natural": 2,
     "turned0": 0,
     "turned1": 2,
-    "turned2": 1,
+    "late0": 1,
     "dealt1": 0,
-    "turned3": 3,
-    "scores00": 4,
-    "scores01": 5,
+    "late1": 3,
+    "scores0": 4,
     "slots0": 6,
     "slots1": 7,
     "slots2": 2,
@@ -59,8 +64,6 @@ BANK = {
     "y01": 5,
     "y10": 0,
     "y11": 1,
-    "y12": 3,
-    "y13": 6,
 }
 
 
@@ -94,7 +97,7 @@ def tile_attend_mla_kernel(tc, qT, cT, ts, ch, offs, out):
         nc.sync.dma_start(out=ch_sb[:], in_=ch)
 
         toks = [over.tile([P, N], F32, name=f"toks{b}", align_bytes=64, offset=TOKS_AT[b]) for b in range(B)]
-        parts = keep.tile([P, B, PACK], F32, name="parts")
+        parts = keep.tile([P, B, len(EXP_RUNS)], F32, name="parts")
         total = keep.tile([P, B], F32, name="total")
         inv = keep.tile([P, B], F32, name="inv")
         made = {}
@@ -121,7 +124,7 @@ def tile_attend_mla_kernel(tc, qT, cT, ts, ch, offs, out):
             return late(f"keys{b}", N * PACK, BF16)
 
         def vals(b, g):
-            return late(f"vals{b}{g}", DV * len(GROUPS[b][g]), BF16)
+            return late(f"vals{b}{g}", 2 * DV, BF16)
 
         def codes(kind, b, width):
             return late(f"{kind}q{b}", width, U32), late(f"{kind}s{b}", width, U8)
@@ -161,22 +164,26 @@ def tile_attend_mla_kernel(tc, qT, cT, ts, ch, offs, out):
             )
 
         def tv(b, t):
-            turned = bank(f"turned{t}")[:].rearrange("s (b u p) -> s b u p", b=B, u=2)
+            name, at = (f"turned{t}", b) if t < 2 else (f"late{b}", t - 2)
+            turned = bank(name)[:].rearrange("s (x u p) -> s x u p", x=2, u=2)
             words = picked(b, t // 2)[:, (t % 2) * N : (t % 2 + 1) * N].bitcast(F32).rearrange("p (s u) -> p u s", u=2)
             for u in range(2):
-                nc.tensor.transpose(turned[:, b, u, :], words[:, u, :], ident[:])
+                nc.tensor.transpose(turned[:, at, u, :], words[:, u, :], ident[:])
 
-        def vc(b, g, e):
-            count = len(GROUPS[b][g])
+        def vc(b, t):
             nc.scalar.copy(
-                out=vals(b, g)[:].bitcast(F32).rearrange("s (c e p u) -> s e c p u", c=CUTS[b], e=count, u=2)[:, e],
-                in_=bank(f"turned{GROUPS[b][g][e]}")[:].rearrange("s (b u c p) -> s b c p u", b=B, u=2, c=CUTS[b])[:, b],
+                out=vals(b, t // 2)[:].bitcast(F32).rearrange("s (c e p u) -> s e c p u", c=2, e=2, u=2)[:, t % 2],
+                in_=bank(f"turned{t}")[:].rearrange("s (b u c p) -> s b c p u", b=B, u=2, c=2)[:, b],
             )
 
-        def qv(b, c, g):
-            width = len(GROUPS[b][g]) * P // CUTS[b]
-            first = c * DV // CUTS[b] + GROUPS[b][g][0] * P // CUTS[b]
-            quantise("v", b, DV, slice(first, first + width), vals(b, g)[:, c * width * PACK : (c + 1) * width * PACK])
+        def vc_late(b):
+            nc.scalar.copy(
+                out=vals(b, 1)[:].bitcast(F32).rearrange("s (c e p u) -> s c e p u", c=2, e=2, u=2),
+                in_=bank(f"late{b}")[:].rearrange("s (e u c p) -> s c e p u", e=2, u=2, c=2),
+            )
+
+        def qv(b, g):
+            quantise(f"v{g}", b, HALF, slice(0, HALF), vals(b, g)[:])
 
         def qc(b):
             nc.scalar.copy(
@@ -190,8 +197,8 @@ def tile_attend_mla_kernel(tc, qT, cT, ts, ch, offs, out):
         def qK(b, first, count):
             quantise("k", b, N, slice(first, first + count), keys(b)[:, PACK * first : PACK * (first + count)])
 
-        def mm(b, h):
-            product(bank(f"scores{b}{h}", HALF)[:], codes("q", b, NQ), slice(0, NQ), codes("k", b, N), slice(h * HALF, (h + 1) * HALF))
+        def mm0():
+            product(bank("scores0")[:], codes("q", 0, NQ), slice(0, NQ), codes("k", 0, N), slice(0, N))
 
         def mm1(j):
             product(bank(f"slots{j}", NQ)[:], codes("k", 1, N), slice(j * P, (j + 1) * P), codes("q", 1, NQ), slice(0, NQ))
@@ -223,12 +230,11 @@ def tile_attend_mla_kernel(tc, qT, cT, ts, ch, offs, out):
         def spc(b):
             nc.scalar.copy(out=late(f"trow{b}", N, F32)[:], in_=bank(f"spread{b}")[:])
 
-        def sca(b, h):
-            part = slice(h * P // 2, (h + 1) * P // 2)
+        def sca0():
             nc.vector.tensor_tensor(
-                out=late(f"a{b}s", N, F32)[:].rearrange("q (j s) -> q j s", j=PACK)[:, :, part],
-                in0=bank(f"scores{b}{h}")[:].rearrange("q (s j) -> q j s", j=PACK),
-                in1=late(f"trow{b}", N, F32)[:].rearrange("q (j s) -> q j s", j=PACK)[:, :, part],
+                out=late("a0s", N, F32)[:].rearrange("q (j s) -> q j s", j=PACK),
+                in0=bank("scores0")[:].rearrange("q (s j) -> q j s", j=PACK),
+                in1=late("trow0", N, F32)[:].rearrange("q (j s) -> q j s", j=PACK),
                 op=ALU.mult,
             )
 
@@ -274,11 +280,6 @@ def tile_attend_mla_kernel(tc, qT, cT, ts, ch, offs, out):
         def qw(b):
             quantise("w", b, NQ, slice(0, NQ), late(f"w{b}", NQ * PACK, BF16)[:])
 
-        def row_sum(b):
-            nc.scalar.activation(
-                out=total[:, b : b + 1], in_=parts[:, b, 0:1], func=ACT.Identity, bias=parts[:, b, 1:2], scale=1.0
-            )
-
         def row_sums():
             nc.vector.tensor_reduce(out=total[:], in_=parts[:], axis=mybir.AxisListType.X, op=ALU.add)
 
@@ -286,23 +287,21 @@ def tile_attend_mla_kernel(tc, qT, cT, ts, ch, offs, out):
             nc.vector.reciprocal(out=inv[:], in_=total[:])
 
         def mix(b, c):
-            width = DV // CUTS[b]
-            product(bank(f"y{b}{c}", width)[:], codes("w", b, NQ), slice(0, NQ), codes("v", b, DV), slice(c * width, (c + 1) * width))
+            for g in range(2):
+                dst = bank(f"y{b}{c}", HALF)[:, g * P : (g + 1) * P]
+                product(dst, codes("w", b, NQ), slice(0, NQ), codes(f"v{g}", b, HALF), slice(c * P, (c + 1) * P))
 
-        def fin(b, c):
-            width = DV // CUTS[b]
-            cols = slice(c * width, (c + 1) * width)
+        def fin(b, c, first=0, count=HALF):
+            cols = slice(c * HALF + first, c * HALF + first + count)
             nc.vector.scalar_tensor_tensor(
                 out=late(f"o{b}", DV, F32)[:, cols].rearrange("q (p t) -> q p t", t=PACK),
-                in0=bank(f"y{b}{c}")[:].rearrange("q (t p) -> q p t", t=PACK),
+                in0=bank(f"y{b}{c}")[:].rearrange("q (t p) -> q p t", t=PACK)[:, first // PACK : (first + count) // PACK, :],
                 scalar=inv[:, b : b + 1],
                 in1=ch_sb[:, cols].rearrange("q (p t) -> q p t", t=PACK),
                 op0=ALU.mult,
                 op1=ALU.mult,
             )
-
-        def store(b, first, count):
-            nc.sync.dma_start(out=out[b][:, first : first + count], in_=late(f"o{b}", DV, F32)[:, first : first + count])
+            nc.sync.dma_start(out=out[b][:, cols], in_=late(f"o{b}", DV, F32)[:, cols])
 
         tok(0)
         tok1()
@@ -317,21 +316,19 @@ def tile_attend_mla_kernel(tc, qT, cT, ts, ch, offs, out):
         tv(1, 0)
         gather(0, 1, 0, N, False)
         gather(1, 1, 0, N, True)
-        vc(0, 0, 0)
-        vc(1, 0, 0)
+        vc(0, 0)
+        vc(1, 0)
         spc(0)
         weave(0, 0, 0, N)
         weave(1, 0, 0, N)
         tv(0, 1)
         tv(1, 1)
-        vc(0, 1, 0)
-        vc(1, 0, 1)
+        vc(0, 1)
+        vc(1, 1)
         tt("dealt1", toks[1][:].rearrange("q (s j) -> q j s", j=PACK))
-        qv(0, 0, 0)
-        qv(0, 1, 0)
-        qv(0, 0, 1)
-        qv(0, 1, 1)
-        for c in range(PACK): qv(1, c, 0)
+        tcl("dealt1", "tcol1")
+        qv(0, 0)
+        qv(1, 0)
         gather(0, 2, 0, N, False)
         gather(1, 2, 0, N, True)
         tv(0, 2)
@@ -352,23 +349,20 @@ def tile_attend_mla_kernel(tc, qT, cT, ts, ch, offs, out):
         weave(1, 1, 0, HALF)
         qK(0, 0, N)
         qQ(0)
-        mm(0, 0)
-        mm(0, 1)
+        mm0()
         weave(1, 1, HALF, P)
         qK(1, 0, P)
         qQ(1)
         mm1(0)
         qK(1, P, P)
         mm1(1)
-        tcl("dealt1", "tcol1")
-        vc(0, 2, 0)
-        vc(0, 3, 0)
+        vc_late(0)
         qK(1, 2 * P, P)
         mm1(2)
         qK(1, 3 * P, P)
         mm1(3)
-        sca(0, 0)
-        sca(0, 1)
+        sca0()
+        qv(0, 1)
         mx(0)
         sca1(0)
         ta(0)
@@ -378,33 +372,24 @@ def tile_attend_mla_kernel(tc, qT, cT, ts, ch, offs, out):
         ta(2)
         sca1(3)
         ta(3)
-        vc(1, 1, 0)
-        vc(1, 1, 1)
+        vc_late(1)
         mx(1)
-        for j in range(PACK): ex(0, j, j, 1)
-        for j in range(PACK): ex(1, j, j, 1)
+        for b in range(B):
+            for part, (first, count) in enumerate(EXP_RUNS):
+                ex(b, part, first, count)
+        qv(1, 1)
         w(0)
+        row_sums()
         qw(0)
-        w(1)
-        qw(1)
-        qv(0, 0, 2)
-        qv(0, 1, 2)
-        qv(0, 0, 3)
-        qv(0, 1, 3)
+        rec()
         mix(0, 0)
         mix(0, 1)
-        for c in range(PACK): qv(1, c, 1)
-        row_sums()
-        rec()
-        for c in range(PACK): mix(1, c)
+        w(1)
         fin(0, 0)
-        store(0, 0, HALF)
+        qw(1)
         fin(0, 1)
-        store(0, HALF, HALF)
+        mix(1, 0)
+        mix(1, 1)
         fin(1, 0)
-        fin(1, 1)
-        store(1, 0, HALF)
-        fin(1, 2)
-        store(1, HALF, P)
-        fin(1, 3)
-        store(1, 3 * P, P)
+        fin(1, 1, 0, P)
+        fin(1, 1, P, P)

@@ -25,21 +25,18 @@ PLANE_AT = [8 * KB * t for t in range(PACK)]
 QRAW_AT = [32 * KB, 36 * KB]
 TOKS_AT = [44 * KB + 2 * KB * b for b in range(B)]
 SPARE_AT = 48 * KB
-SCALED_AT = 54 * KB
-ROW_AT = 56 * KB
 COLUMN_AT = 60 * KB
+RESULT_AT = 62 * KB
 LIES_ON = {
     "picked10": TOKS_AT[0],
     "vals00": SPARE_AT,
     "picked1": SPARE_AT,
     "q_sb1": PLANE_AT[3] + KB,
     "vals01": QRAW_AT[1],
-    "scaled3": SCALED_AT,
-    "v1s1": SCALED_AT,
     "tcol0": COLUMN_AT,
     "w1": COLUMN_AT,
-    "keys1": ROW_AT,
-    "v1s0": ROW_AT,
+    "tcol1": RESULT_AT,
+    "o0": RESULT_AT,
     "kq1": QRAW_AT[0],
     "vals11": QRAW_AT[0],
 }
@@ -183,7 +180,9 @@ def tile_attend_mla_kernel(tc, qT, cT, ts, ch, offs, out):
             )
 
         def qv(b, g):
-            quantise(f"v{g}", b, HALF, slice(0, HALF), vals(b, g)[:])
+            for c in range(2):
+                first = c * HALF + g * P
+                quantise("v", b, DV, slice(first, first + P), vals(b, g)[:, c * DV : (c + 1) * DV])
 
         def qc(b):
             nc.scalar.copy(
@@ -287,9 +286,7 @@ def tile_attend_mla_kernel(tc, qT, cT, ts, ch, offs, out):
             nc.vector.reciprocal(out=inv[:], in_=total[:])
 
         def mix(b, c):
-            for g in range(2):
-                dst = bank(f"y{b}{c}", HALF)[:, g * P : (g + 1) * P]
-                product(dst, codes("w", b, NQ), slice(0, NQ), codes(f"v{g}", b, HALF), slice(c * P, (c + 1) * P))
+            product(bank(f"y{b}{c}", HALF)[:], codes("w", b, NQ), slice(0, NQ), codes("v", b, DV), slice(c * HALF, (c + 1) * HALF))
 
         def fin(b, c, first=0, count=HALF):
             cols = slice(c * HALF + first, c * HALF + first + count)
@@ -314,12 +311,14 @@ def tile_attend_mla_kernel(tc, qT, cT, ts, ch, offs, out):
         tcl("natural", "tnat")
         tv(0, 0)
         tv(1, 0)
-        gather(0, 1, 0, N, False)
+        gather(0, 1, 0, HALF, False)
+        gather(0, 1, HALF, HALF, False)
         gather(1, 1, 0, N, True)
         vc(0, 0)
         vc(1, 0)
         spc(0)
-        weave(0, 0, 0, N)
+        weave(0, 0, 0, HALF)
+        weave(0, 0, HALF, HALF)
         weave(1, 0, 0, N)
         tv(0, 1)
         tv(1, 1)
@@ -381,12 +380,12 @@ def tile_attend_mla_kernel(tc, qT, cT, ts, ch, offs, out):
         w(0)
         row_sums()
         qw(0)
-        rec()
         mix(0, 0)
         mix(0, 1)
         w(1)
-        fin(0, 0)
+        rec()
         qw(1)
+        fin(0, 0)
         fin(0, 1)
         mix(1, 0)
         mix(1, 1)

@@ -27,6 +27,7 @@ TOKS_AT = [44 * KB + 2 * KB * b for b in range(B)]
 SPARE_AT = 48 * KB
 COLUMN_AT = 60 * KB
 RESULT_AT = 62 * KB
+SCALED_AT = 54 * KB
 LIES_ON = {
     "picked10": TOKS_AT[0],
     "vals00": SPARE_AT,
@@ -37,6 +38,8 @@ LIES_ON = {
     "w1": COLUMN_AT,
     "tcol1": RESULT_AT,
     "o0": RESULT_AT,
+    "scaled3": SCALED_AT,
+    "vs1": SCALED_AT,
     "kq1": QRAW_AT[0],
     "vals11": QRAW_AT[0],
 }
@@ -327,7 +330,6 @@ def tile_attend_mla_kernel(tc, qT, cT, ts, ch, offs, out):
         tt("dealt1", toks[1][:].rearrange("q (s j) -> q j s", j=PACK))
         tcl("dealt1", "tcol1")
         qv(0, 0)
-        qv(1, 0)
         gather(0, 2, 0, N, False)
         gather(1, 2, 0, N, True)
         tv(0, 2)
@@ -376,6 +378,7 @@ def tile_attend_mla_kernel(tc, qT, cT, ts, ch, offs, out):
         for b in range(B):
             for part, (first, count) in enumerate(EXP_RUNS):
                 ex(b, part, first, count)
+        qv(1, 0)
         qv(1, 1)
         w(0)
         row_sums()

from contextlib import ExitStack

import concourse.mybir as mybir
from concourse.masks import make_identity

B, N, T, D, DV, NQ = 2, 512, 2048, 512, 512, 128
P = 128
PACK = 4
HALF = N // 2
FLOPS = 2 * B * NQ * N * (D + DV)

F32 = mybir.dt.float32
BF16 = mybir.dt.bfloat16
U32 = mybir.dt.uint32
U16 = mybir.dt.uint16
U8 = mybir.dt.uint8
FP8X4 = mybir.dt.float8_e4m3fn_x4
ACT = mybir.ActivationFunctionType
ALU = mybir.AluOpType

HEAD = 512
KB = 1024
EXP_RUNS = [(0, 2), (2, 1), (3, 1)]
PLANE_AT = [8 * KB * t for t in range(PACK)]
QRAW_AT = [32 * KB, 36 * KB]
TOKS_AT = [44 * KB + 2 * KB * b for b in range(B)]
SPARE_AT = 48 * KB
COLUMN_AT = 60 * KB
RESULT_AT = 62 * KB
SCALED_AT = 54 * KB
LIES_ON = {
    "picked10": TOKS_AT[0],
    "vals00": SPARE_AT,
    "picked1": SPARE_AT,
    "q_sb1": PLANE_AT[3] + KB,
    "vals01": QRAW_AT[1],
    "tcol0": COLUMN_AT,
    "w1": COLUMN_AT,
    "tcol1": RESULT_AT,
    "o0": RESULT_AT,
    "scaled3": SCALED_AT,
    "vs1": SCALED_AT,
    "kq1": QRAW_AT[0],
    "vals11": QRAW_AT[0],
}
BANK = {
    "dealt0": 0,
    "spread0": 1,
    "natural": 2,
    "turned0": 0,
    "turned1": 2,
    "late0": 1,
    "dealt1": 0,
    "late1": 3,
    "scores0": 4,
    "slots0": 6,
    "slots1": 7,
    "slots2": 2,
    "slots3": 0,
    "a1": 6,
    "pt0": 7,
    "pt1": 2,
    "y00": 4,
    "y01": 5,
    "y10": 0,
    "y11": 1,
}


def tile_attend_mla_kernel(tc, qT, cT, ts, ch, offs, out):
    nc = tc.nc
    with ExitStack() as ctx:
        keep = ctx.enter_context(tc.tile_pool(name="keep", bufs=1))
        over = ctx.enter_context(tc.tile_pool(name="over", bufs=1))
        psum = ctx.enter_context(tc.psum_pool(name="psum", bufs=1))

        ts_sb = keep.tile([P, T], F32, name="ts_sb")
        nc.gpsimd.memset(ts_sb[0 : P - 1, 1536:T], 0.0)
        nc.vector.memset(ts_sb[0 : P - 1, 0:1535], 0.0)
        nc.vector.memset(ts_sb[0 : P - 1, 1535:1536], 0.0)
        ident = keep.tile([P, P], F32, name="ident")
        make_identity(nc, ident[:])

        offsets = keep.tile([P, B * N // 16], U16, name="offsets")
        nc.sync.dma_start(offsets[:], offs)
        nc.sync.dma_start(out=ts_sb[P - 1 : P, :], in_=ts[0:1, :])
        pool_rows = cT.rearrange("(p t) n -> p t n", t=PACK)
        planes = [over.tile([P, T], F32, name=f"plane{t}", align_bytes=64, offset=PLANE_AT[t]) for t in range(PACK)]
        nc.scalar.dma_start(out=planes[0][:, :HEAD], in_=pool_rows[:, 0, :HEAD])
        nc.sync.dma_start(out=planes[0][:, HEAD:], in_=pool_rows[:, 0, HEAD:])
        for t in range(1, PACK):
            nc.sync.dma_start(out=planes[t][:], in_=pool_rows[:, t, :])
        q_raw = [over.tile([P, PACK, NQ], F32, name=f"q_raw{b}", align_bytes=64, offset=QRAW_AT[b]) for b in range(B)]
        for b in range(B):
            nc.sync.dma_start(out=q_raw[b][:], in_=qT[b].rearrange("(p t) q -> p t q", t=PACK))
        ch_sb = keep.tile([P, DV], F32, name="ch_sb")
        nc.sync.dma_start(out=ch_sb[:], in_=ch)

        toks = [over.tile([P, N], F32, name=f"toks{b}", align_bytes=64, offset=TOKS_AT[b]) for b in range(B)]
        parts = keep.tile([P, B, len(EXP_RUNS)], F32, name="parts")
        total = keep.tile([P, B], F32, name="total")
        inv = keep.tile([P, B], F32, name="inv")
        made = {}

        def late(name, width, dt):
            if name not in made:
                if name in LIES_ON:
                    made[name] = over.tile([P, width], dt, name=name, align_bytes=64, offset=LIES_ON[name])
                else:
                    made[name] = keep.tile([P, width], dt, name=name, align_bytes=64)
            return made[name]

        def bank(name, width=N):
            if name not in made:
                made[name] = psum.tile([P, width], F32, name=name, tag=f"bank{BANK[name]}")
            return made[name]

        def picked(b, u):
            if u == 0:
                return late(f"picked{b}0", 2 * N, BF16)
            return late("picked1", B * 2 * N, BF16)[:, b * 2 * N : (b + 1) * 2 * N]

        def keys(b):
            return late(f"keys{b}", N * PACK, BF16)

        def vals(b, g):
            return late(f"vals{b}{g}", 2 * DV, BF16)

        def codes(kind, b, width):
            return late(f"{kind}q{b}", width, U32), late(f"{kind}s{b}", width, U8)

        def quantise(kind, b, width, cols, src):
            words, scales = codes(kind, b, width)
            nc.vector.quantize_mx(out=words[:, cols].bitcast(FP8X4), scales=scales[:, cols], in_=src)

        def product(dst, left, left_cols, right, right_cols):
            nc.tensor.matmul_mx(
                out=dst,
                lhsT=left[0][:, left_cols].bitcast(FP8X4),
                lhsT_scale=left[1][:, left_cols],
                rhs=right[0][:, right_cols].bitcast(FP8X4),
                rhs_scale=right[1][:, right_cols],
                start=True,
                stop=True,
            )

        def entries(b, first, count):
            col = (b * N + first) // 16
            return offsets[:, col : col + count // 16]

        def gather(b, t, first, count, on_scalar):
            at = (t % 2) * N + first
            dst = picked(b, t // 2)[:, at : at + count]
            src = planes[t][:].indirect(entries(b, first, count))
            if on_scalar:
                nc.scalar.activation(out=dst, in_=src, func=ACT.Copy)
            else:
                nc.vector.tensor_copy(out=dst, in_=src)

        def weave(b, u, first, count, on_scalar=False):
            (nc.scalar.copy if on_scalar else nc.vector.tensor_copy)(
                out=keys(b)[:].rearrange("p (n t) -> p n t", t=PACK)[:, first : first + count, 2 * u : 2 * u + 2],
                in_=picked(b, u)[:, :].rearrange("p (e n) -> p n e", e=2)[:, first : first + count, :],
            )

        def tv(b, t):
            name, at = (f"turned{t}", b) if t < 2 else (f"late{b}", t - 2)
            turned = bank(name)[:].rearrange("s (x u p) -> s x u p", x=2, u=2)
            words = picked(b, t // 2)[:, (t % 2) * N : (t % 2 + 1) * N].bitcast(F32).rearrange("p (s u) -> p u s", u=2)
            for u in range(2):
                nc.tensor.transpose(turned[:, at, u, :], words[:, u, :], ident[:])

        def vc(b, t):
            nc.scalar.copy(
                out=vals(b, t // 2)[:].bitcast(F32).rearrange("s (c e p u) -> s e c p u", c=2, e=2, u=2)[:, t % 2],
                in_=bank(f"turned{t}")[:].rearrange("s (b u c p) -> s b c p u", b=B, u=2, c=2)[:, b],
            )

        def vc_late(b):
            nc.scalar.copy(
                out=vals(b, 1)[:].bitcast(F32).rearrange("s (c e p u) -> s c e p u", c=2, e=2, u=2),
                in_=bank(f"late{b}")[:].rearrange("s (e u c p) -> s c e p u", e=2, u=2, c=2),
            )

        def qv(b, g):
            for c in range(2):
                first = c * HALF + g * P
                quantise("v", b, DV, slice(first, first + P), vals(b, g)[:, c * DV : (c + 1) * DV])

        def qc(b):
            nc.scalar.copy(
                out=late(f"q_sb{b}", NQ * PACK, BF16)[:].rearrange("p (c i t) -> p c t i", i=4, t=PACK),
                in_=q_raw[b][:].rearrange("p t (c i) -> p c t i", i=4),
            )

        def qQ(b):
            quantise("q", b, NQ, slice(0, NQ), late(f"q_sb{b}", NQ * PACK, BF16)[:])

        def qK(b, first, count):
            quantise("k", b, N, slice(first, first + count), keys(b)[:, PACK * first : PACK * (first + count)])

        def mm0():
            product(bank("scores0")[:], codes("q", 0, NQ), slice(0, NQ), codes("k", 0, N), slice(0, N))

        def mm1(j):
            product(bank(f"slots{j}", NQ)[:], codes("k", 1, N), slice(j * P, (j + 1) * P), codes("q", 1, NQ), slice(0, NQ))

        def tok(b):
            nc.vector.tensor_copy(
                out=toks[b][:].bitcast(U32).rearrange("q (j s) -> q s j", j=PACK),
                in_=ts_sb[:].bitcast(U32).indirect(entries(b, 0, N)),
            )

        def tok1():
            nc.vector.tensor_copy(out=toks[1][:], in_=ts_sb[:].indirect(entries(1, 0, N)))

        def tt(name, src):
            for j in range(PACK):
                nc.tensor.transpose(bank(name)[:, j * P : (j + 1) * P], src[:, j, :], ident[:])

        def tcl(name, col):
            nc.scalar.activation(
                out=late(col, PACK, F32)[:], in_=bank(name)[:].rearrange("s (j q) -> s j q", j=PACK)[:, :, P - 1], func=ACT.Copy
            )

        def spt(b):
            for j in range(PACK):
                nc.tensor.transpose(
                    bank(f"spread{b}")[:, j * P : (j + 1) * P], late(f"tcol{b}", PACK, F32)[:, j : j + 1].to_broadcast([P, P]), ident[:]
                )

        def spc(b):
            nc.scalar.copy(out=late(f"trow{b}", N, F32)[:], in_=bank(f"spread{b}")[:])

        def sca0():
            nc.vector.tensor_tensor(
                out=late("a0s", N, F32)[:].rearrange("q (j s) -> q j s", j=PACK),
                in0=bank("scores0")[:].rearrange("q (s j) -> q j s", j=PACK),
                in1=late("trow0", N, F32)[:].rearrange("q (j s) -> q j s", j=PACK),
                op=ALU.mult,
            )

        def sca1(j):
            nc.scalar.activation(
                out=late(f"scaled{j}", NQ, F32)[:], in_=bank(f"slots{j}")[:], func=ACT.Copy, scale=late("tnat", PACK, F32)[:, j : j + 1]
            )

        def ta(j):
            nc.tensor.transpose(bank("a1")[:, j * P : (j + 1) * P], late(f"scaled{j}", NQ, F32)[:], ident[:])

        def a(b):
            if b:
                return bank("a1")[:].rearrange("q (s j) -> q j s", j=PACK)
            return late(f"a{b}s", N, F32)[:].rearrange("q (j s) -> q j s", j=PACK)

        def mx(b):
            nc.vector.tensor_reduce(
                out=late(f"neg_m{b}", 1, F32)[:], in_=bank("a1")[:] if b else late("a0s", N, F32)[:], axis=mybir.AxisListType.X, op=ALU.max, negate=True
            )

        def ex(b, part, first, count):
            nc.scalar.activation(
                out=late(f"p{b}", N, F32)[:].rearrange("q (j s) -> q j s", j=PACK)[:, first : first + count, :],
                in_=a(b)[:, first : first + count, :],
                func=ACT.Exp,
                bias=late(f"neg_m{b}", 1, F32)[:],
                scale=1.0,
                accum_out=parts[:, b, part : part + 1],
            )
            for j in range(first, first + count):
                cols = slice(j * P, (j + 1) * P)
                nc.tensor.transpose(bank(f"pt{b}")[:, cols], late(f"p{b}", N, F32)[:, cols], ident[:])

        def w(b):
            nc.vector.tensor_tensor(
                out=late(f"w{b}", NQ * PACK, BF16)[:].rearrange("s (q j) -> s q j", j=PACK),
                in0=bank(f"pt{b}")[:].rearrange("s (j q) -> s q j", j=PACK),
                in1=late(f"tcol{b}", PACK, F32)[:].unsqueeze(1).to_broadcast([P, NQ, PACK]),
                op=ALU.mult,
            )

        def qw(b):
            quantise("w", b, NQ, slice(0, NQ), late(f"w{b}", NQ * PACK, BF16)[:])

        def row_sums():
            nc.vector.tensor_reduce(out=total[:], in_=parts[:], axis=mybir.AxisListType.X, op=ALU.add)

        def rec():
            nc.vector.reciprocal(out=inv[:], in_=total[:])

        def mix(b, c):
            product(bank(f"y{b}{c}", HALF)[:], codes("w", b, NQ), slice(0, NQ), codes("v", b, DV), slice(c * HALF, (c + 1) * HALF))

        def fin(b, c, first=0, count=HALF):
            cols = slice(c * HALF + first, c * HALF + first + count)
            nc.vector.scalar_tensor_tensor(
                out=late(f"o{b}", DV, F32)[:, cols].rearrange("q (p t) -> q p t", t=PACK),
                in0=bank(f"y{b}{c}")[:].rearrange("q (t p) -> q p t", t=PACK)[:, first // PACK : (first + count) // PACK, :],
                scalar=inv[:, b : b + 1],
                in1=ch_sb[:, cols].rearrange("q (p t) -> q p t", t=PACK),
                op0=ALU.mult,
                op1=ALU.mult,
            )
            nc.sync.dma_start(out=out[b][:, cols], in_=late(f"o{b}", DV, F32)[:, cols])

        tok(0)
        tok1()
        tt("dealt0", toks[0][:].rearrange("q (j s) -> q j s", j=PACK))
        tcl("dealt0", "tcol0")
        spt(0)
        tt("natural", toks[1][:].rearrange("q (j s) -> q j s", j=PACK))
        gather(0, 0, 0, N, False)
        gather(1, 0, 0, N, True)
        tcl("natural", "tnat")
        tv(0, 0)
        tv(1, 0)
        gather(0, 1, 0, HALF, False)
        gather(0, 1, HALF, HALF, False)
        gather(1, 1, 0, N, True)
        vc(0, 0)
        vc(1, 0)
        spc(0)
        weave(0, 0, 0, HALF)
        weave(0, 0, HALF, HALF)
        weave(1, 0, 0, N)
        tv(0, 1)
        tv(1, 1)
        vc(0, 1)
        vc(1, 1)
        tt("dealt1", toks[1][:].rearrange("q (s j) -> q j s", j=PACK))
        tcl("dealt1", "tcol1")
        qv(0, 0)
        gather(0, 2, 0, N, False)
        gather(1, 2, 0, N, True)
        tv(0, 2)
        tv(1, 2)
        gather(0, 3, 0, P, False)
        gather(0, 3, P, P, False)
        gather(0, 3, HALF, HALF, True)
        gather(1, 3, 0, HALF, True)
        gather(1, 3, HALF, HALF, True)
        qc(0)
        qc(1)
        weave(1, 1, 3 * P, P, True)
        tv(0, 3)
        tv(1, 3)
        weave(0, 1, 0, P)
        weave(0, 1, P, P)
        weave(0, 1, HALF, HALF)
        weave(1, 1, 0, HALF)
        qK(0, 0, N)
        qQ(0)
        mm0()
        weave(1, 1, HALF, P)
        qK(1, 0, P)
        qQ(1)
        mm1(0)
        qK(1, P, P)
        mm1(1)
        vc_late(0)
        qK(1, 2 * P, P)
        mm1(2)
        qK(1, 3 * P, P)
        mm1(3)
        sca0()
        qv(0, 1)
        mx(0)
        sca1(0)
        ta(0)
        sca1(1)
        ta(1)
        sca1(2)
        ta(2)
        sca1(3)
        ta(3)
        vc_late(1)
        mx(1)
        for b in range(B):
            for part, (first, count) in enumerate(EXP_RUNS):
                ex(b, part, first, count)
        qv(1, 0)
        qv(1, 1)
        w(0)
        row_sums()
        qw(0)
        mix(0, 0)
        mix(0, 1)
        w(1)
        rec()
        qw(1)
        fin(0, 0)
        fin(0, 1)
        mix(1, 0)
        mix(1, 1)
        fin(1, 0)
        fin(1, 1, 0, P)
        fin(1, 1, P, P)
